import numpy as np, ml_dtypes
CORES = [2,3,42,43,82,83,122,123]
N = 8
import mx_ref
BF = ml_dtypes.bfloat16
def entries(a):
    return np.ascontiguousarray(a.T).reshape(-1)
def table(e):
    return np.ascontiguousarray(np.reshape(e, (-1, 16)).T).astype(np.int32)
def cols(t, e):
    v = np.concatenate([t.reshape(128, -1, 4), np.zeros((128, 1, 4), BF)], axis=1)
    return np.ascontiguousarray(v[:, e]).reshape(128, -1)
def f(rng, *shape):
    return mx_ref.flush((rng.standard_normal(shape, dtype=np.float32) * np.exp2(rng.integers(-2, 3, shape[:-1] + (1,)))).astype(BF))
def wide(rng, *shape, cols=0):
    v = rng.standard_normal(shape, dtype=np.float32) * np.exp2(rng.integers(-12, 13, shape)).astype(np.float32)
    if cols: v *= np.repeat(np.exp2(rng.integers(-cols, cols + 1, shape[:-2] + (1, shape[-1] // 4))) * (rng.random(shape[:-2] + (1, shape[-1] // 4)) > 0.0625), 4, axis=-1).astype(np.float32)
    return mx_ref.flush(v.astype(BF))
T, S, CAPP = 512, 256, 48
def lists(rng, most=None, own=False, share=False, edge=False):
    o, c, m = [], [], []
    for r in range(N):
        n = np.zeros(N, int)
        if own: n[r] = CAPP
        if most is not None:
            for q in rng.permutation(N)[:most]: n[q] = CAPP
            n = np.minimum(n, np.maximum(0, S - (np.cumsum(n) - n)))
        while n.sum() < S:
            q = rng.integers(0, N)
            if n[q] < CAPP: n[q] += 1
        slots = np.full(N * CAPP, -1); used = []
        for q in range(N):
            k = q * CAPP + rng.permutation(CAPP)[:n[q]]; used += list(k)
            slots[k] = rng.integers(0, T) if share else rng.choice([0, T - 1], n[q]) if edge else rng.integers(0, T, n[q])
        o.append(table(rng.choice([0, T - 1], S) if edge else rng.integers(0, T, S))); c.append(table(slots)); m.append(table(rng.permutation(used)))
    return {"own": np.stack(o), "want": np.stack(c), "slot": np.stack(m)}
def setup_inputs(rng):
    return {"x": f(rng, N, 128, 4 * T), "w": f(rng, N, 128, 512), **lists(rng)}
def setup_inputs_edge(rng):
    return {**setup_inputs(rng), **lists(rng, edge=True)}
def setup_inputs_full(rng):
    return {**setup_inputs(rng), **lists(rng, most=S // CAPP)}
def setup_inputs_self(rng):
    return {**setup_inputs(rng), **lists(rng, own=True)}
def setup_inputs_share(rng):
    return {**setup_inputs(rng), **lists(rng, share=True)}
def setup_inputs_spread(rng):
    d = setup_inputs(rng); d["x"] = wide(rng, N, 128, 4 * T, cols=8); return d
def check_inputs(d):
    b = []
    for r in range(N):
        o, c, m = entries(d["own"][r]), entries(d["want"][r]), entries(d["slot"][r])
        if o.min() < 0 or o.max() >= T: b.append("own")
        if c.min() < -1 or c.max() >= T: b.append("want")
        if m.min() < 0 or m.max() >= N * CAPP or len(set(m.tolist())) != S or (c[m] < 0).any() or (c >= 0).sum() != S: b.append("slot")
    return b
def decode(q):
    out = np.zeros(q[0].shape, np.float32)
    for b in range(4):
        e = np.zeros((128, 128, 4), np.float32); e[np.arange(128), np.arange(128), b] = 1
        out[:, b::4] = mx_ref.matmul(mx_ref.quantize(e.reshape(128, 512).astype(BF)), q)
    return out
def reference(x, w, own, want, slot):
    M = []
    for r in range(N):
        c = entries(want[r])
        arrived = np.concatenate([decode(mx_ref.quantize(cols(x[q], c[q * CAPP:(q + 1) * CAPP]))) for q in range(N)], axis=1)
        far = arrived.reshape(128, -1, 4)[:, entries(slot[r])].reshape(128, -1)
        M.append(mx_ref.quantize(((cols(x[r], entries(own[r])).astype(np.float32) + far) * np.float32(0.5)).astype(BF)))
    y = np.zeros((N, 128, 3 * S), np.float32)
    for r in range(N):
        for i in range(3): y[r][:, S * i:S * i + S] = mx_ref.matmul(mx_ref.quantize(w[r]), M[(r - 1 + i) % N])
    return {"y": y}

@@ -1,0 +1,321 @@
+from concourse.bass import DstId, RemoteDMATransfer
+from concourse.mybir import dt, AluOpType, ActivationFunctionType
+
+CODE = "float8_e4m3fn_x4"
+SCRATCH = {
+    "wantr": ("sbuf", [128, 24], "int32"),
+    "ownr": ("sbuf", [128, 16], "int32"),
+    "slotr": ("sbuf", [128, 16], "int32"),
+    "req": ("sbuf", [128, 24], "uint16"),
+    "selfoff": ("sbuf", [128, 4], "uint16"),
+    "landc": ("sbuf", [128, 12], "uint16"),
+    "landp": ("sbuf", [128, 12], "uint16"),
+    "ownoff": ("sbuf", [128, 16], "uint16"),
+    "slotoff": ("sbuf", [128, 16], "uint16"),
+    "xs": ("sbuf", [128, 2048], "bfloat16"),
+    "ws": ("sbuf", [128, 512], "bfloat16"),
+    "hc": ("sbuf", [128, 768], "bfloat16"),
+    "hp": ("sbuf", [128, 768], "bfloat16"),
+    "qc": ("sbuf", [128, 192], CODE),
+    "qcs": ("sbuf", [128, 192], "uint8"),
+    "qp": ("sbuf", [128, 192], CODE),
+    "qps": ("sbuf", [128, 192], "uint8"),
+    "fc": ("sbuf", [128, 192], CODE),
+    "fcs": ("sbuf", [128, 192], "uint8"),
+    "fp": ("sbuf", [128, 192], CODE),
+    "fps": ("sbuf", [128, 192], "uint8"),
+    "diff": ("sbuf", [128, 128], "int32"),
+    "ez": ("sbuf", [128, 2048], "bfloat16"),
+    "eq": ("sbuf", [128, 512], CODE),
+    "eqs": ("sbuf", [128, 512], "uint8"),
+    "wq": ("sbuf", [128, 128], CODE),
+    "wqs": ("sbuf", [128, 128], "uint8"),
+    "acol": ("sbuf", [128, 1024], "bfloat16"),
+    "fcol": ("sbuf", [128, 1536], "bfloat16"),
+    "h": ("sbuf", [128, 1024], "bfloat16"),
+    "mq": ("sbuf", [128, 256], CODE),
+    "mqs": ("sbuf", [128, 256], "uint8"),
+    "onq": ("sbuf", [128, 256], CODE),
+    "onqs": ("sbuf", [128, 256], "uint8"),
+    "offq": ("sbuf", [128, 256], CODE),
+    "offqs": ("sbuf", [128, 256], "uint8"),
+    "ysb": ("sbuf", [128, 768], "float32"),
+}
+for _i in range(8):
+    SCRATCH["st%d" % _i] = ("sbuf", [128, 16], "int32")
+for _i in range(4):
+    SCRATCH["pc%d" % _i] = ("psum", [128, 512], "float32")
+    SCRATCH["pp%d" % _i] = ("psum", [128, 512], "float32")
+
+SEMAPHORES = (["ldwant", "ldx", "ldw", "ldown", "ldslot", "iota", "zero", "vreq", "vself", "ve", "veq", "vwq", "lstc", "lstp",
+               "vc", "sc", "vp", "sp", "qcd", "qpd", "selfd", "fcd", "fpd", "vown", "va", "sa", "vslot",
+               "vf", "sf", "vh0", "vh1", "m0", "m1", "mon", "moff", "mmw", "mmn", "mmf0", "mmf1",
+               "yw", "yn", "yf0", "yf1", "stw", "stn", "stf0", "stf1", "loc"]
+              + ["mmc%d" % i for i in range(4)] + ["mmp%d" % i for i in range(4)])
+
+
+def rank_program(g, core, T, topo):
+    r = T.rank_of(core)
+    if r is None:
+        return
+    N, CAP, S = 8, 48, 256
+    LC = CAP // 16
+    A, COPY = AluOpType, ActivationFunctionType.Copy
+    V, SC, SY, PE, sem = g.vector, g.scalar, g.sync, g.tensor, T.sem
+    cores = T.cores
+    chip = [topo.chip(c) for c in cores]
+
+    def groups(q):
+        cross = [s for s in range(N) if chip[s] != chip[q] and not topo.same_plane(chip[s], chip[q])]
+        return cross, [s for s in range(N) if s not in cross]
+
+    cross, near = groups(r)
+    mate = [s for s in near if s != r and chip[s] == chip[r]][0]
+    plane = [s for s in near if chip[s] != chip[r]]
+    asks = [s for s in near if s != r]
+    prv, nxt = (r - 1) % N, (r + 1) % N
+    offn = prv if nxt == mate else nxt
+    off = topo.engines(core, cores[cross[0]])
+    on = [e for e in topo.engines(core, cores[mate]) if e not in off][:4]
+
+    def bits(es):
+        return sum(1 << e for e in es)
+
+    def part(i, n):
+        k = len(off) // n
+        return off[i * k:(i + 1) * k]
+
+    sent = [0]
+
+    def write(d, es, src, dst, rsem):
+        rid, pid = topo.addr(cores[d])[:2]
+        sent[0] += len(es)
+        return RemoteDMATransfer(dst_ids=[DstId(rid=rid, pnc=pid)], dma_engine_mask=bits(es), remote_sem=rsem,
+                                 srcs=[src], dsts=[dst])
+
+    def fused(ts):
+        g.remote_dma_fused(ts, local_sem=sem.loc)
+
+    def u8(ap):
+        return ap.bitcast(dt.uint8)
+
+    for k in range(8):
+        (SY if k % 2 == 0 else SC).dma_start(T.wantr[16 * k:16 * k + 16, :], T.want[:]).then_inc(sem.ldwant, 16)
+    SY.dma_start(T.xs[:], T.x[:]).then_inc(sem.ldx, 16)
+    for k in range(8):
+        SY.dma_start(T.ownr[16 * k:16 * k + 16, :], T.own[:]).then_inc(sem.ldown, 16)
+    SY.dma_start(T.ws[:], T.w[:]).then_inc(sem.ldw, 16)
+    for k in range(8):
+        SY.dma_start(T.slotr[16 * k:16 * k + 16, :], T.slot[:]).then_inc(sem.ldslot, 16)
+
+    g.iota(T.diff[:], [[1, 128]], 0, -1).then_inc(sem.iota, 1)
+    V.memset(T.ez[:], 0.0).then_inc(sem.zero, 1)
+    V.wait_ge(sem.ldwant, 128)
+    V.tensor_scalar(T.req[:], T.wantr[:], 4, 0, A.mult, A.max).then_inc(sem.vreq, 1)
+    V.tensor_scalar(T.selfoff[:, 0:LC], T.wantr[:, LC * r:LC * r + LC], 4, 0, A.mult, A.max).then_inc(sem.vself, 1)
+
+    def reqs(q):
+        return T.req[:, LC * q:LC * q + LC]
+
+    g.wait_ge(sem.vreq, 1)
+    ts = []
+    for i, q in enumerate(cross):
+        k = groups(q)[0].index(r)
+        ts.append(write(q, part(i, len(cross)), reqs(q), T.landc[:, LC * k:LC * k + LC], sem.lstc))
+    fused(ts)
+    ts = []
+    for q in plane + [mate]:
+        k = [s for s in groups(q)[1] if s != q].index(r)
+        es = on if q == mate else part(plane.index(q), len(plane))
+        ts.append(write(q, es, reqs(q), T.landp[:, LC * k:LC * k + LC], sem.lstp))
+    fused(ts)
+
+    V.wait_ge(sem.iota, 1)
+    V.wait_ge(sem.zero, 1)
+    for b in range(4):
+        V.tensor_scalar(T.ez[:, 512 * b + b:512 * b + 512:4], T.diff[:], 0, 0.5, A.is_equal, A.mult).then_inc(sem.ve, 1)
+    V.wait_ge(sem.ve, 4)
+    V.quantize_mx(T.eq[:], T.eqs[:], T.ez[:]).then_inc(sem.veq, 1)
+
+    def gather(eng, out, off_ap, t, s):
+        src = T.xs[:, t:2048].indirect(off_ap)
+        if eng == "v":
+            V.tensor_copy(out, src).then_inc(s, 1)
+        else:
+            SC.activation(out, src, COPY).then_inc(s, 1)
+
+    for eng, q, s in (("v", V, "v"), ("s", SC, "s")):
+        tt = (0, 1) if eng == "v" else (2, 3)
+        q.wait_ge(sem.vself, 1)
+        q.wait_ge(sem.ldx, 16)
+        for t in tt:
+            gather(eng, T.hp[:, t:4 * CAP:4], T.selfoff[:, 0:LC], t, sem[s + "p"])
+        q.wait_ge(sem.lstc, len(off))
+        for t in tt:
+            gather(eng, T.hc[:, t:768:4], T.landc[:, 0:4 * LC], t, sem[s + "c"])
+        if eng == "v":
+            V.wait_ge(sem.vc, 2)
+            V.wait_ge(sem.sc, 2)
+            V.quantize_mx(T.qc[:], T.qcs[:], T.hc[:]).then_inc(sem.qcd, 1)
+        q.wait_ge(sem.lstp, len(off) + len(on))
+        for t in tt:
+            gather(eng, T.hp[:, 4 * CAP + t:768:4], T.landp[:, 0:3 * LC], t, sem[s + "p"])
+        if eng == "v":
+            V.wait_ge(sem.vp, 4)
+            V.wait_ge(sem.sp, 4)
+            V.quantize_mx(T.qp[:], T.qps[:], T.hp[:]).then_inc(sem.qpd, 1)
+
+    for w4 in (4, 1):
+        if w4 == 4:
+            g.wait_ge(sem.qcd, 1)
+        ts = []
+        for i, q in enumerate(cross):
+            k, a = groups(q)[0].index(r), CAP * i
+            if w4 == 4:
+                src, dst = u8(T.qc[:, a:a + CAP]), u8(T.fc[:, CAP * k:CAP * k + CAP])
+            else:
+                src, dst = T.qcs[:, a:a + CAP], T.fcs[:, CAP * k:CAP * k + CAP]
+            ts.append(write(q, part(i, len(cross)), src, dst, sem.fcd))
+        fused(ts)
+    for w4 in (4, 1):
+        if w4 == 4:
+            g.wait_ge(sem.qpd, 1)
+        ts = []
+        for q in plane + [mate]:
+            k, a = groups(q)[1].index(r), CAP * (1 + asks.index(q))
+            es = on if q == mate else part(plane.index(q), len(plane))
+            if w4 == 4:
+                src, dst = u8(T.qp[:, a:a + CAP]), u8(T.fp[:, CAP * k:CAP * k + CAP])
+            else:
+                src, dst = T.qps[:, a:a + CAP], T.fps[:, CAP * k:CAP * k + CAP]
+            ts.append(write(q, es, src, dst, sem.fpd))
+        fused(ts)
+    ks = CAP * near.index(r)
+    SY.wait_ge(sem.qpd, 1)
+    SY.dma_start(u8(T.fp[:, ks:ks + CAP]), u8(T.qp[:, 0:CAP])).then_inc(sem.selfd, 16)
+    SY.dma_start(T.fps[:, ks:ks + CAP], T.qps[:, 0:CAP]).then_inc(sem.selfd, 16)
+
+    V.wait_ge(sem.ldown, 128)
+    V.tensor_scalar(T.ownoff[:], T.ownr[:], 4, None, A.mult).then_inc(sem.vown, 1)
+    V.wait_ge(sem.vown, 1)
+    SC.wait_ge(sem.vown, 1)
+    for t in range(2):
+        V.tensor_scalar(T.acol[:, S * t:S * t + S], T.xs[:, t:2048].indirect(T.ownoff[:]), 0.5, None, A.mult).then_inc(sem.va, 1)
+    for t in range(2, 4):
+        SC.activation(T.acol[:, S * t:S * t + S], T.xs[:, t:2048].indirect(T.ownoff[:]), COPY, scale=0.5).then_inc(sem.sa, 1)
+
+    first, second = (cross, near) if 0 in cross else (near, cross)
+    land = first + second
+    base = {"c": CAP * land.index(cross[0]), "p": CAP * land.index(near[0])}
+    steps, prev = [], 0
+    for q in range(1, N):
+        d = CAP * (land.index(q) - q)
+        if d != prev:
+            steps.append((CAP * q, d - prev))
+            prev = d
+    V.wait_ge(sem.ldslot, 128)
+    n = 0
+    terms = [T.slotr]
+    for j, (at, d) in enumerate(steps):
+        V.tensor_scalar(T["st%d" % j][:], T.slotr[:], at, d, A.is_ge, A.mult).then_inc(sem.vslot, 1)
+        terms.append(T["st%d" % j])
+        n += 1
+    fresh = len(steps)
+    while len(terms) > 1:
+        V.wait_ge(sem.vslot, n)
+        nxt_terms = []
+        for j in range(0, len(terms) - 1, 2):
+            o = T["st%d" % fresh]
+            fresh += 1
+            V.tensor_tensor(o[:], terms[j][:], terms[j + 1][:], A.add).then_inc(sem.vslot, 1)
+            n += 1
+            nxt_terms.append(o)
+        if len(terms) % 2:
+            nxt_terms.append(terms[-1])
+        terms = nxt_terms
+    V.wait_ge(sem.vslot, n)
+    V.tensor_copy(T.slotoff[:], terms[0][:]).then_inc(sem.vslot, 1)
+    n += 1
+    V.wait_ge(sem.ldw, 16)
+    V.quantize_mx(T.wq[:], T.wqs[:], T.ws[:]).then_inc(sem.vwq, 1)
+
+    PE.wait_ge(sem.veq, 1)
+    order = (0, 2, 1, 3)
+    for c, wide in (("c", 192), ("p", 192)):
+        if c == "c":
+            PE.wait_ge(sem.fcd, 2 * len(off))
+        else:
+            PE.wait_ge(sem.selfd, 32)
+            PE.wait_ge(sem.fpd, 2 * (len(off) + len(on)))
+        codes, scales = (T.fc, T.fcs) if c == "c" else (T.fp, T.fps)
+        for b in order:
+            PE.matmul_mx(T["p%s%d" % (c, b)][:, 0:wide], T.eq[:, 128 * b:128 * b + 128], T.eqs[:, 128 * b:128 * b + 128],
+                         codes[:, 0:wide], scales[:, 0:wide], True, True).then_inc(sem["mm%s%d" % (c, b)], 1)
+        for b in range(4):
+            o = T.fcol[:, 384 * b + base[c]:384 * b + base[c] + wide]
+            src = T["p%s%d" % (c, b)][:, 0:wide]
+            if b < 2:
+                V.wait_ge(sem["mm%s%d" % (c, b)], 1)
+                V.tensor_copy(o, src).then_inc(sem.vf, 1)
+            else:
+                SC.wait_ge(sem["mm%s%d" % (c, b)], 1)
+                SC.activation(o, src, COPY).then_inc(sem.sf, 1)
+
+    V.wait_ge(sem.vslot, n)
+    V.wait_ge(sem.va, 2)
+    V.wait_ge(sem.sa, 2)
+    V.wait_ge(sem.vf, 4)
+    for hf in range(2):
+        for t in range(4):
+            if hf == 0 and t == 2:
+                V.wait_ge(sem.sf, 4)
+            V.tensor_tensor(T.h[:, 512 * hf + t:512 * hf + 512:4],
+                            T.fcol[:, 384 * t:384 * t + 384].indirect(T.slotoff[:, 8 * hf:8 * hf + 8]),
+                            T.acol[:, S * t + 128 * hf:S * t + 128 * hf + 128], A.add).then_inc(sem["vh%d" % hf], 1)
+        V.wait_ge(sem["vh%d" % hf], 4)
+        V.quantize_mx(T.mq[:, 128 * hf:128 * hf + 128], T.mqs[:, 128 * hf:128 * hf + 128],
+                      T.h[:, 512 * hf:512 * hf + 512]).then_inc(sem["m%d" % hf], 1)
+        g.wait_ge(sem["m%d" % hf], 1)
+        a, b = 128 * hf, 128 * hf + 128
+        fused([write(offn, off, u8(T.mq[:, a:b]), u8(T.offq[:, a:b]), sem.moff),
+               write(mate, on, u8(T.mq[:, a:b]), u8(T.onq[:, a:b]), sem.mon)])
+    fused([write(offn, off, T.mqs[:], T.offqs[:], sem.moff), write(mate, on, T.mqs[:], T.onqs[:], sem.mon)])
+
+    sec = {prv: 0, r: 1, nxt: 2}
+
+    def ycols(q, a, b):
+        return slice(S * sec[q] + a, S * sec[q] + b)
+
+    PE.wait_ge(sem.vwq, 1)
+    PE.wait_ge(sem.m0, 1)
+    PE.wait_ge(sem.m1, 1)
+    PE.matmul_mx(T.pc0[:, 0:S], T.wq[:], T.wqs[:], T.mq[:], T.mqs[:], True, True).then_inc(sem.mmw, 1)
+    PE.wait_ge(sem.mon, 3 * len(on))
+    PE.matmul_mx(T.pc1[:, 0:S], T.wq[:], T.wqs[:], T.onq[:], T.onqs[:], True, True).then_inc(sem.mmn, 1)
+    PE.wait_ge(sem.moff, 3 * len(off))
+    PE.matmul_mx(T.pc2[:, 0:128], T.wq[:], T.wqs[:], T.offq[:, 0:128], T.offqs[:, 0:128], True, True).then_inc(sem.mmf0, 1)
+    PE.matmul_mx(T.pc3[:, 0:128], T.wq[:], T.wqs[:], T.offq[:, 128:256], T.offqs[:, 128:256], True, True).then_inc(sem.mmf1, 1)
+
+    V.wait_ge(sem.mmw, 1)
+    V.tensor_copy(T.ysb[:, ycols(r, 0, S)], T.pc0[:, 0:S]).then_inc(sem.yw, 1)
+    SC.wait_ge(sem.mmn, 1)
+    SC.activation(T.ysb[:, ycols(mate, 0, S)], T.pc1[:, 0:S], COPY).then_inc(sem.yn, 1)
+    V.wait_ge(sem.mmf0, 1)
+    V.tensor_copy(T.ysb[:, ycols(offn, 0, 128)], T.pc2[:, 0:128]).then_inc(sem.yf0, 1)
+    SC.wait_ge(sem.mmf1, 1)
+    SC.activation(T.ysb[:, ycols(offn, 128, S)], T.pc3[:, 0:128], COPY).then_inc(sem.yf1, 1)
+
+    SY.wait_ge(sem.yw, 1)
+    SY.dma_start(T.y[:, ycols(r, 0, S)], T.ysb[:, ycols(r, 0, S)]).then_inc(sem.stw, 16)
+    SY.wait_ge(sem.yn, 1)
+    SY.dma_start(T.y[:, ycols(mate, 0, S)], T.ysb[:, ycols(mate, 0, S)]).then_inc(sem.stn, 16)
+    SY.wait_ge(sem.yf0, 1)
+    SY.dma_start(T.y[:, ycols(offn, 0, 128)], T.ysb[:, ycols(offn, 0, 128)]).then_inc(sem.stf0, 16)
+    SC.wait_ge(sem.yf1, 1)
+    SC.dma_start(T.y[:, ycols(offn, 128, S)], T.ysb[:, ycols(offn, 128, S)]).then_inc(sem.stf1, 16)
+
+    g.wait_ge(sem.loc, sent[0])
+    SY.wait_ge(sem.stw, 16)
+    SY.wait_ge(sem.stn, 16)
+    SY.wait_ge(sem.stf0, 16)
+    SC.wait_ge(sem.stf1, 16)

@@ -4,54 +4,73 @@ from concourse.mybir import dt, AluOpType, ActivationFunctionType
 CODE = "float8_e4m3fn_x4"
 SCRATCH = {
     "wantr": ("sbuf", [128, 24], "int32"),
-    "ownr": ("sbuf", [128, 16], "int32"),
     "slotr": ("sbuf", [128, 16], "int32"),
     "req": ("sbuf", [128, 24], "uint16"),
     "selfoff": ("sbuf", [128, 4], "uint16"),
-    "landc": ("sbuf", [128, 12], "uint16"),
-    "landp": ("sbuf", [128, 12], "uint16"),
-    "ownoff": ("sbuf", [128, 16], "uint16"),
+    "la": ("sbuf", [128, 8], "uint16"),
+    "lb": ("sbuf", [128, 16], "uint16"),
+    "lp": ("sbuf", [128, 8], "uint16"),
+    "slotown": ("sbuf", [128, 16], "uint16"),
+    "sloton": ("sbuf", [128, 16], "uint16"),
     "slotoff": ("sbuf", [128, 16], "uint16"),
+    "hi": ("sbuf", [128, 16], "int32"),
+    "hi2": ("sbuf", [128, 16], "int32"),
+    "s24": ("sbuf", [128, 16], "int32"),
+    "place": ("sbuf", [128, 32], "float32"),
+    "placet": ("sbuf", [128, 32], "float32"),
+    "placeu": ("sbuf", [128, 16], "uint16"),
+    "ownrow": ("sbuf", [128, 256], "int32"),
+    "invrow": ("sbuf", [128, 384], "int32"),
+    "invw": ("sbuf", [128, 24], "int32"),
+    "inv": ("sbuf", [128, 24], "uint16"),
     "xs": ("sbuf", [128, 2048], "bfloat16"),
     "ws": ("sbuf", [128, 512], "bfloat16"),
-    "hc": ("sbuf", [128, 768], "bfloat16"),
-    "hp": ("sbuf", [128, 768], "bfloat16"),
-    "qc": ("sbuf", [128, 192], CODE),
-    "qcs": ("sbuf", [128, 192], "uint8"),
-    "qp": ("sbuf", [128, 192], CODE),
-    "qps": ("sbuf", [128, 192], "uint8"),
-    "fc": ("sbuf", [128, 192], CODE),
-    "fcs": ("sbuf", [128, 192], "uint8"),
-    "fp": ("sbuf", [128, 192], CODE),
-    "fps": ("sbuf", [128, 192], "uint8"),
+    "ha": ("sbuf", [128, 512], "bfloat16"),
+    "hb": ("sbuf", [128, 768], "bfloat16"),
+    "hp": ("sbuf", [128, 512], "bfloat16"),
+    "f1": ("sbuf", [128, 224], CODE),
+    "f1s": ("sbuf", [128, 224], "uint8"),
+    "f2": ("sbuf", [128, 336], CODE),
+    "f2s": ("sbuf", [128, 336], "uint8"),
+    "f3": ("sbuf", [128, 224], CODE),
+    "f3s": ("sbuf", [128, 224], "uint8"),
     "diff": ("sbuf", [128, 128], "int32"),
-    "ez": ("sbuf", [128, 2048], "bfloat16"),
+    "ez": ("sbuf", [128, 520], "bfloat16"),
     "eq": ("sbuf", [128, 512], CODE),
     "eqs": ("sbuf", [128, 512], "uint8"),
     "wq": ("sbuf", [128, 128], CODE),
     "wqs": ("sbuf", [128, 128], "uint8"),
-    "acol": ("sbuf", [128, 1024], "bfloat16"),
-    "fcol": ("sbuf", [128, 1536], "bfloat16"),
-    "h": ("sbuf", [128, 1024], "bfloat16"),
-    "mq": ("sbuf", [128, 256], CODE),
-    "mqs": ("sbuf", [128, 256], "uint8"),
-    "onq": ("sbuf", [128, 256], CODE),
-    "onqs": ("sbuf", [128, 256], "uint8"),
-    "offq": ("sbuf", [128, 256], CODE),
-    "offqs": ("sbuf", [128, 256], "uint8"),
+    "acol": ("sbuf", [128, 1536], "bfloat16"),
+    "h": ("sbuf", [128, 1536], "bfloat16"),
+    "m1": ("sbuf", [128, 192], CODE),
+    "m1s": ("sbuf", [128, 192], "uint8"),
+    "m2": ("sbuf", [128, 128], CODE),
+    "m2s": ("sbuf", [128, 128], "uint8"),
+    "m3": ("sbuf", [128, 128], CODE),
+    "m3s": ("sbuf", [128, 128], "uint8"),
+    "onq": ("sbuf", [128, 384], CODE),
+    "onqs": ("sbuf", [128, 384], "uint8"),
+    "offq": ("sbuf", [128, 384], CODE),
+    "offqs": ("sbuf", [128, 384], "uint8"),
+    "yown": ("sbuf", [128, 384], "float32"),
+    "yon": ("sbuf", [128, 384], "float32"),
+    "yoff": ("sbuf", [128, 384], "float32"),
     "ysb": ("sbuf", [128, 768], "float32"),
 }
 for _i in range(8):
-    SCRATCH["st%d" % _i] = ("sbuf", [128, 16], "int32")
-for _i in range(4):
-    SCRATCH["pc%d" % _i] = ("psum", [128, 512], "float32")
-    SCRATCH["pp%d" % _i] = ("psum", [128, 512], "float32")
+    SCRATCH["ps%d" % _i] = ("psum", [128, 512], "float32")
 
-SEMAPHORES = (["ldwant", "ldx", "ldw", "ldown", "ldslot", "iota", "zero", "vreq", "vself", "ve", "veq", "vwq", "lstc", "lstp",
-               "vc", "sc", "vp", "sp", "qcd", "qpd", "selfd", "fcd", "fpd", "vown", "va", "sa", "vslot",
-               "vf", "sf", "vh0", "vh1", "m0", "m1", "mon", "moff", "mmw", "mmn", "mmf0", "mmf1",
-               "yw", "yn", "yf0", "yf1", "stw", "stn", "stf0", "stf1", "loc"]
-              + ["mmc%d" % i for i in range(4)] + ["mmp%d" % i for i in range(4)])
+GROUPS = "agbp"
+YS = ("own1", "own2", "own3", "on1", "off1", "on2", "off2", "on3", "off3")
+PICKS = ("own", "on", "offa", "offb")
+SEMAPHORES = (["ldwant", "ldx", "ldw", "ldown", "ldslot", "ldinv", "iota", "iota0", "zero", "vreq", "vself", "ve", "veq", "vwq",
+               "vslot", "k1", "k2", "k3", "k4", "k5", "scat", "vinv", "gself", "lston", "lstoff", "m1", "m2", "m3", "loc"]
+              + [k + c for c in "abp" for k in ("lst", "gv", "gs", "q")]
+              + [k + c for c in GROUPS for k in ("fd", "add")]
+              + ["own%d%d" % (i, t) for i in (1, 2) for t in range(4)]
+              + ["mm%s%d" % (c, b) for c in GROUPS for b in range(4)]
+              + [k + y for y in YS for k in ("l", "y", "c")]
+              + [k + y for y in PICKS for k in ("pk", "st")])
 
 
 def rank_program(g, core, T, topo):
@@ -60,29 +79,56 @@ def rank_program(g, core, T, topo):
         return
     N, CAP, S = 8, 48, 256
     LC = CAP // 16
+    G = 2 * CAP
+    W = N * CAP
     A, COPY = AluOpType, ActivationFunctionType.Copy
     V, SC, SY, PE, sem = g.vector, g.scalar, g.sync, g.tensor, T.sem
     cores = T.cores
     chip = [topo.chip(c) for c in cores]
+    chips = sorted(set(chip), key=chip.index)
+    first = {}
+    for c in chips:
+        if c not in first:
+            d = [d for d in chips if d != c and d not in first and not topo.same_plane(c, d)][0]
+            first[c], first[d] = d, c
+
+    def ranks(c):
+        return [s for s in range(N) if chip[s] == c]
 
     def groups(q):
-        cross = [s for s in range(N) if chip[s] != chip[q] and not topo.same_plane(chip[s], chip[q])]
-        return cross, [s for s in range(N) if s not in cross]
+        c = chip[q]
+        return {"a": ranks(first[c]), "g": ranks(c),
+                "b": [s for s in range(N) if chip[s] not in (c, first[c]) and not topo.same_plane(chip[s], c)],
+                "p": [s for s in range(N) if topo.same_plane(chip[s], c)]}
 
-    cross, near = groups(r)
-    mate = [s for s in near if s != r and chip[s] == chip[r]][0]
-    plane = [s for s in near if chip[s] != chip[r]]
-    asks = [s for s in near if s != r]
+    def pieces(q):
+        gq = groups(q)
+        return [(CAP * min(gq["a"] + gq["g"]), 2 * G), (CAP * gq["b"][0], G), (CAP * gq["p"][0], G)]
+
+    grp = groups(r)
+    mate = [s for s in grp["g"] if s != r][0]
     prv, nxt = (r - 1) % N, (r + 1) % N
     offn = prv if nxt == mate else nxt
-    off = topo.engines(core, cores[cross[0]])
-    on = [e for e in topo.engines(core, cores[mate]) if e not in off][:4]
+    off = topo.engines(core, cores[grp["a"][0]])
+    on = [e for e in topo.engines(core, cores[mate]) if e not in off]
+
+    def pos(q):
+        return ranks(chip[q]).index(q)
+
+    def lay(q):
+        if pos(q) == 0:
+            return {"tile": 0, "askb": 0, "askm": G, "own": G + CAP, "mate": 2 * G, "landb": 2 * G + CAP,
+                    "wing": (2 * G + CAP - 128, 32), "winb": (2 * G + CAP - 32, 32), "listb": 0, "listm": 2 * LC}
+        return {"landb": 0, "mate": G, "tile": G + CAP, "own": G + CAP, "askm": 2 * G, "askb": 2 * G + CAP,
+                "wing": (G, 0), "winb": (0, 0), "listm": 0, "listb": LC}
+
+    L = lay(r)
 
     def bits(es):
         return sum(1 << e for e in es)
 
-    def part(i, n):
-        k = len(off) // n
+    def half(i):
+        k = len(off) // 2
         return off[i * k:(i + 1) * k]
 
     sent = [0]
@@ -96,226 +142,239 @@ def rank_program(g, core, T, topo):
     def fused(ts):
         g.remote_dma_fused(ts, local_sem=sem.loc)
 
-    def u8(ap):
-        return ap.bitcast(dt.uint8)
+    def piece(name, plane, a, n):
+        return T[name + "s"][:, a:a + n] if plane else T[name][:, a:a + n].bitcast(dt.uint8)
 
-    for k in range(8):
-        (SY if k % 2 == 0 else SC).dma_start(T.wantr[16 * k:16 * k + 16, :], T.want[:]).then_inc(sem.ldwant, 16)
+    for k, q in enumerate((SY, SC)):
+        q.dma_start(T.wantr[16 * k:16 * k + 16, :], T.want[:]).then_inc(sem.ldwant, 16)
+        q.dma_start(T.slotr[16 * k:16 * k + 16, :], T.slot[:]).then_inc(sem.ldslot, 16)
     SY.dma_start(T.xs[:], T.x[:]).then_inc(sem.ldx, 16)
-    for k in range(8):
-        SY.dma_start(T.ownr[16 * k:16 * k + 16, :], T.own[:]).then_inc(sem.ldown, 16)
+    SC.wait_ge(sem.iota0, 1)
+    SY.wait_ge(sem.iota0, 1)
+    for k, q in enumerate((SC, SC, SY, SC)):
+        q.dma_start(T.ownrow[16 * k:16 * k + 1, :], T.own[:]).then_inc(sem.ldown, 16)
     SY.dma_start(T.ws[:], T.w[:]).then_inc(sem.ldw, 16)
-    for k in range(8):
-        SY.dma_start(T.slotr[16 * k:16 * k + 16, :], T.slot[:]).then_inc(sem.ldslot, 16)
+    blocks = [slice(32 * k, 32 * k + 32) for k in range(4)]
 
+    def make_e(b):
+        V.quantize_mx(T.eq[:, 128 * b:128 * b + 128], T.eqs[:, 128 * b:128 * b + 128],
+                      T.ez[:, 3 - b:515 - b]).then_inc(sem.veq, 1)
+
+    g.iota(T.ownrow[:], [[0, S]], 0, 0).then_inc(sem.iota0, 1)
     g.iota(T.diff[:], [[1, 128]], 0, -1).then_inc(sem.iota, 1)
     V.memset(T.ez[:], 0.0).then_inc(sem.zero, 1)
-    V.wait_ge(sem.ldwant, 128)
-    V.tensor_scalar(T.req[:], T.wantr[:], 4, 0, A.mult, A.max).then_inc(sem.vreq, 1)
-    V.tensor_scalar(T.selfoff[:, 0:LC], T.wantr[:, LC * r:LC * r + LC], 4, 0, A.mult, A.max).then_inc(sem.vself, 1)
+    V.memset(T.ha[:, 4 * G:512], 0.0).then_inc(sem.zero, 1)
+    V.memset(T.hp[:, 4 * G:512], 0.0).then_inc(sem.zero, 1)
+    V.memset(T.invrow[:], 0).then_inc(sem.zero, 1)
+    V.wait_ge(sem.ldwant, 32)
+    for b in blocks:
+        V.tensor_scalar(T.req[b, :], T.wantr[0:32, :], 4, 0, A.mult, A.max).then_inc(sem.vreq, 1)
+    V.wait_ge(sem.iota, 1)
+    V.wait_ge(sem.zero, 4)
+    V.tensor_scalar(T.ez[:, 3:515:4], T.diff[:], 0, 0.5, A.is_equal, A.mult).then_inc(sem.ve, 1)
+    V.wait_ge(sem.vreq, 4)
+    V.tensor_copy(T.selfoff[:, 0:LC], T.req[:, LC * r:LC * r + LC]).then_inc(sem.vself, 1)
+    V.wait_ge(sem.ve, 1)
+
+    b0 = blocks[0]
+    V.wait_ge(sem.ldslot, 32)
+    V.tensor_scalar(T.hi[b0, :], T.slotr[b0, :], 4, None, A.arith_shift_right).then_inc(sem.k1, 1)
+    V.tensor_scalar(T.s24[b0, :], T.slotr[b0, :], W // 16, None, A.mult).then_inc(sem.k2, 1)
+    V.wait_ge(sem.k1, 1)
+    V.tensor_scalar(T.hi2[b0, :], T.hi[b0, :], 1 - W, None, A.mult).then_inc(sem.k2, 1)
+    make_e(0)
+    V.wait_ge(sem.k2, 2)
+    for k in range(2):
+        V.tensor_tensor(T.place[b0, 16 * k:16 * k + 16], T.s24[b0, :], T.hi2[b0, :], A.add).then_inc(sem.k3, 1)
+    V.wait_ge(sem.k3, 2)
+    V.transpose(T.placet[b0, :], T.place[b0, :]).then_inc(sem.k4, 1)
+    make_e(1)
+    V.wait_ge(sem.k4, 1)
+    for b in blocks:
+        V.tensor_copy(T.placeu[b, :], T.placet[b0, 0:16]).then_inc(sem.k5, 1)
+    V.wait_ge(sem.k5, 4)
+    V.wait_ge(sem.ldown, 64)
+    V.tensor_copy(T.invrow[:].indirect(T.placeu[:]), T.ownrow[:]).then_inc(sem.scat, 1)
+    SY.wait_ge(sem.scat, 1)
+    SY.dma_start(T.invw[0:64, :], T.invrow[0:64:16, :]).then_inc(sem.ldinv, 16)
+    for b in blocks:
+        V.tensor_copy(T.slotown[b, :], T.slotr[b0, :]).then_inc(sem.vslot, 1)
+    make_e(2)
+    make_e(3)
 
     def reqs(q):
         return T.req[:, LC * q:LC * q + LC]
 
-    g.wait_ge(sem.vreq, 1)
-    ts = []
-    for i, q in enumerate(cross):
-        k = groups(q)[0].index(r)
-        ts.append(write(q, part(i, len(cross)), reqs(q), T.landc[:, LC * k:LC * k + LC], sem.lstc))
-    fused(ts)
-    ts = []
-    for q in plane + [mate]:
-        k = [s for s in groups(q)[1] if s != q].index(r)
-        es = on if q == mate else part(plane.index(q), len(plane))
-        ts.append(write(q, es, reqs(q), T.landp[:, LC * k:LC * k + LC], sem.lstp))
-    fused(ts)
+    g.wait_ge(sem.vreq, 4)
+    for c in "abp":
+        ts = []
+        for i, q in enumerate(grp[c]):
+            k = LC * pos(r) + (lay(q)["listb"] if c == "b" else 0)
+            ts.append(write(q, half(i), reqs(q), T["l" + c][:, k:k + LC], sem["lst" + c]))
+        if c == "b":
+            k = lay(mate)["listm"]
+            ts.append(write(mate, on, reqs(mate), T.lb[:, k:k + LC], sem.lstb))
+        fused(ts)
+    g.wait_ge(sem.vslot, 4)
+    fused([write(offn, off, T.slotown[:], T.slotoff[:], sem.lstoff), write(mate, on, T.slotown[:], T.sloton[:], sem.lston)])
 
-    V.wait_ge(sem.iota, 1)
-    V.wait_ge(sem.zero, 1)
-    for b in range(4):
-        V.tensor_scalar(T.ez[:, 512 * b + b:512 * b + 512:4], T.diff[:], 0, 0.5, A.is_equal, A.mult).then_inc(sem.ve, 1)
-    V.wait_ge(sem.ve, 4)
-    V.quantize_mx(T.eq[:], T.eqs[:], T.ez[:]).then_inc(sem.veq, 1)
-
-    def gather(eng, out, off_ap, t, s):
-        src = T.xs[:, t:2048].indirect(off_ap)
+    def gather(eng, out, src, s, scale=None):
         if eng == "v":
-            V.tensor_copy(out, src).then_inc(s, 1)
-        else:
+            if scale is None:
+                V.tensor_copy(out, src).then_inc(s, 1)
+            else:
+                V.tensor_scalar(out, src, scale, None, A.mult).then_inc(s, 1)
+        elif scale is None:
             SC.activation(out, src, COPY).then_inc(s, 1)
+        else:
+            SC.activation(out, src, COPY, scale=scale).then_inc(s, 1)
 
-    for eng, q, s in (("v", V, "v"), ("s", SC, "s")):
-        tt = (0, 1) if eng == "v" else (2, 3)
-        q.wait_ge(sem.vself, 1)
-        q.wait_ge(sem.ldx, 16)
-        for t in tt:
-            gather(eng, T.hp[:, t:4 * CAP:4], T.selfoff[:, 0:LC], t, sem[s + "p"])
-        q.wait_ge(sem.lstc, len(off))
-        for t in tt:
-            gather(eng, T.hc[:, t:768:4], T.landc[:, 0:4 * LC], t, sem[s + "c"])
-        if eng == "v":
-            V.wait_ge(sem.vc, 2)
-            V.wait_ge(sem.sc, 2)
-            V.quantize_mx(T.qc[:], T.qcs[:], T.hc[:]).then_inc(sem.qcd, 1)
-        q.wait_ge(sem.lstp, len(off) + len(on))
-        for t in tt:
-            gather(eng, T.hp[:, 4 * CAP + t:768:4], T.landp[:, 0:3 * LC], t, sem[s + "p"])
-        if eng == "v":
-            V.wait_ge(sem.vp, 4)
-            V.wait_ge(sem.sp, 4)
-            V.quantize_mx(T.qp[:], T.qps[:], T.hp[:]).then_inc(sem.qpd, 1)
+    def xcols(t, offs):
+        return T.xs[:, t:2048].indirect(offs)
 
-    for w4 in (4, 1):
-        if w4 == 4:
-            g.wait_ge(sem.qcd, 1)
-        ts = []
-        for i, q in enumerate(cross):
-            k, a = groups(q)[0].index(r), CAP * i
-            if w4 == 4:
-                src, dst = u8(T.qc[:, a:a + CAP]), u8(T.fc[:, CAP * k:CAP * k + CAP])
-            else:
-                src, dst = T.qcs[:, a:a + CAP], T.fcs[:, CAP * k:CAP * k + CAP]
-            ts.append(write(q, part(i, len(cross)), src, dst, sem.fcd))
-        fused(ts)
-    for w4 in (4, 1):
-        if w4 == 4:
-            g.wait_ge(sem.qpd, 1)
-        ts = []
-        for q in plane + [mate]:
-            k, a = groups(q)[1].index(r), CAP * (1 + asks.index(q))
-            es = on if q == mate else part(plane.index(q), len(plane))
-            if w4 == 4:
-                src, dst = u8(T.qp[:, a:a + CAP]), u8(T.fp[:, CAP * k:CAP * k + CAP])
-            else:
-                src, dst = T.qps[:, a:a + CAP], T.fps[:, CAP * k:CAP * k + CAP]
-            ts.append(write(q, es, src, dst, sem.fpd))
-        fused(ts)
-    ks = CAP * near.index(r)
-    SY.wait_ge(sem.qpd, 1)
-    SY.dma_start(u8(T.fp[:, ks:ks + CAP]), u8(T.qp[:, 0:CAP])).then_inc(sem.selfd, 16)
-    SY.dma_start(T.fps[:, ks:ks + CAP], T.qps[:, 0:CAP]).then_inc(sem.selfd, 16)
+    pc = pieces(r)
+    halves = {1: pc[0][0], 2: min(pc[1][0], pc[2][0])}
 
-    V.wait_ge(sem.ldown, 128)
-    V.tensor_scalar(T.ownoff[:], T.ownr[:], 4, None, A.mult).then_inc(sem.vown, 1)
-    V.wait_ge(sem.vown, 1)
-    SC.wait_ge(sem.vown, 1)
-    for t in range(2):
-        V.tensor_scalar(T.acol[:, S * t:S * t + S], T.xs[:, t:2048].indirect(T.ownoff[:]), 0.5, None, A.mult).then_inc(sem.va, 1)
-    for t in range(2, 4):
-        SC.activation(T.acol[:, S * t:S * t + S], T.xs[:, t:2048].indirect(T.ownoff[:]), COPY, scale=0.5).then_inc(sem.sa, 1)
+    def own_cols(eng, i, t):
+        a = halves[i]
+        gather(eng, T.acol[:, W * t + a:W * t + a + 2 * G], xcols(t, T.inv[:, a // 16:(a + 2 * G) // 16]),
+               sem["own%d%d" % (i, t)], 0.5)
 
-    first, second = (cross, near) if 0 in cross else (near, cross)
-    land = first + second
-    base = {"c": CAP * land.index(cross[0]), "p": CAP * land.index(near[0])}
-    steps, prev = [], 0
-    for q in range(1, N):
-        d = CAP * (land.index(q) - q)
-        if d != prev:
-            steps.append((CAP * q, d - prev))
-            prev = d
-    V.wait_ge(sem.ldslot, 128)
-    n = 0
-    terms = [T.slotr]
-    for j, (at, d) in enumerate(steps):
-        V.tensor_scalar(T["st%d" % j][:], T.slotr[:], at, d, A.is_ge, A.mult).then_inc(sem.vslot, 1)
-        terms.append(T["st%d" % j])
-        n += 1
-    fresh = len(steps)
-    while len(terms) > 1:
-        V.wait_ge(sem.vslot, n)
-        nxt_terms = []
-        for j in range(0, len(terms) - 1, 2):
-            o = T["st%d" % fresh]
-            fresh += 1
-            V.tensor_tensor(o[:], terms[j][:], terms[j + 1][:], A.add).then_inc(sem.vslot, 1)
-            n += 1
-            nxt_terms.append(o)
-        if len(terms) % 2:
-            nxt_terms.append(terms[-1])
-        terms = nxt_terms
-    V.wait_ge(sem.vslot, n)
-    V.tensor_copy(T.slotoff[:], terms[0][:]).then_inc(sem.vslot, 1)
-    n += 1
+    t2 = L["tile"]
+    o2 = 4 * (L["own"] - t2)
+    a2 = 4 * (min(L["askm"], L["askb"]) - t2)
+    SC.wait_ge(sem.vself, 1)
+    SC.wait_ge(sem.ldx, 16)
+    for t in range(4):
+        gather("s", T.hb[:, o2 + t:o2 + 4 * CAP:4], xcols(t, T.selfoff[:, 0:LC]), sem.gself)
+    V.wait_ge(sem.ldx, 16)
+    for eng, q in (("v", V), ("s", SC)):
+        for c in "abp":
+            q.wait_ge(sem["lst" + c], len(off) + (len(on) if c == "b" else 0))
+            for t in ((0, 1) if eng == "v" else (2, 3)):
+                if c == "b":
+                    gather(eng, T.hb[:, a2 + t:a2 + 4 * (G + CAP):4], xcols(t, T.lb[:, 0:3 * LC]), sem["g" + eng + c])
+                else:
+                    gather(eng, T["h" + c][:, t:4 * G:4], xcols(t, T["l" + c][:, 0:2 * LC]), sem["g" + eng + c])
+            if eng == "v":
+                V.wait_ge(sem["gv" + c], 2)
+                V.wait_ge(sem["gs" + c], 2)
+                if c == "b":
+                    V.wait_ge(sem.gself, 4)
+                    V.quantize_mx(T.f2[:, t2:t2 + 2 * G], T.f2s[:, t2:t2 + 2 * G], T.hb[:]).then_inc(sem.qb, 1)
+                else:
+                    f = "f1" if c == "a" else "f3"
+                    V.quantize_mx(T[f][:, 0:128], T[f + "s"][:, 0:128], T["h" + c][:]).then_inc(sem["q" + c], 1)
+    V.wait_ge(sem.ldinv, 16)
+    for k in range(2):
+        V.tensor_scalar(T.inv[64 * k:64 * k + 64, :], T.invw[0:64, :], 4, None, A.mult).then_inc(sem.vinv, 1)
     V.wait_ge(sem.ldw, 16)
     V.quantize_mx(T.wq[:], T.wqs[:], T.ws[:]).then_inc(sem.vwq, 1)
+    V.wait_ge(sem.vinv, 2)
+    own_cols("v", 1, 0)
+    SC.wait_ge(sem.vinv, 2)
+    for i in (1, 2):
+        for t in (1, 2, 3):
+            own_cols("s", i, t)
 
-    PE.wait_ge(sem.veq, 1)
-    order = (0, 2, 1, 3)
-    for c, wide in (("c", 192), ("p", 192)):
-        if c == "c":
-            PE.wait_ge(sem.fcd, 2 * len(off))
-        else:
-            PE.wait_ge(sem.selfd, 32)
-            PE.wait_ge(sem.fpd, 2 * (len(off) + len(on)))
-        codes, scales = (T.fc, T.fcs) if c == "c" else (T.fp, T.fps)
-        for b in order:
-            PE.matmul_mx(T["p%s%d" % (c, b)][:, 0:wide], T.eq[:, 128 * b:128 * b + 128], T.eqs[:, 128 * b:128 * b + 128],
-                         codes[:, 0:wide], scales[:, 0:wide], True, True).then_inc(sem["mm%s%d" % (c, b)], 1)
+    for c in "abp":
+        g.wait_ge(sem["q" + c], 1)
+        for plane in (False, True):
+            ts = []
+            for i, q in enumerate(grp[c]):
+                if c == "b":
+                    src = piece("f2", plane, L["askb"] + CAP * i, CAP)
+                    dst = piece("f2", plane, lay(q)["landb"] + CAP * pos(r), CAP)
+                else:
+                    f = "f1" if c == "a" else "f3"
+                    src, dst = piece(f, plane, CAP * i, CAP), piece(f, plane, 128 + CAP * pos(r), CAP)
+                ts.append(write(q, half(i), src, dst, sem["fd" + c]))
+            if c == "b":
+                ts.append(write(mate, on, piece("f2", plane, L["askm"], CAP),
+                                piece("f2", plane, lay(mate)["mate"], CAP), sem.fdg))
+            fused(ts)
+
+    win = {"a": ("f1", G, 32), "g": ("f2",) + L["wing"], "b": ("f2",) + L["winb"], "p": ("f3", G, 32)}
+    hcol = {"a": CAP * grp["a"][0] - pc[0][0], "g": CAP * grp["g"][0] - pc[0][0], "b": 2 * G, "p": 3 * G}
+    PE.wait_ge(sem.veq, 4)
+    for j, c in enumerate(GROUPS):
+        name, a, skip = win[c]
+        if c != "b":
+            PE.wait_ge(sem["q" + {"a": "a", "g": "b", "p": "p"}[c]], 1)
+        PE.wait_ge(sem["fd" + c], 2 * len(on if c == "g" else off))
+        if j >= 2:
+            PE.wait_ge(sem["add" + GROUPS[j - 2]], 4)
+        at = CAP * grp[c][0]
         for b in range(4):
-            o = T.fcol[:, 384 * b + base[c]:384 * b + base[c] + wide]
-            src = T["p%s%d" % (c, b)][:, 0:wide]
-            if b < 2:
-                V.wait_ge(sem["mm%s%d" % (c, b)], 1)
-                V.tensor_copy(o, src).then_inc(sem.vf, 1)
-            else:
-                SC.wait_ge(sem["mm%s%d" % (c, b)], 1)
-                SC.activation(o, src, COPY).then_inc(sem.sf, 1)
-
-    V.wait_ge(sem.vslot, n)
-    V.wait_ge(sem.va, 2)
-    V.wait_ge(sem.sa, 2)
-    V.wait_ge(sem.vf, 4)
-    for hf in range(2):
-        for t in range(4):
-            if hf == 0 and t == 2:
-                V.wait_ge(sem.sf, 4)
-            V.tensor_tensor(T.h[:, 512 * hf + t:512 * hf + 512:4],
-                            T.fcol[:, 384 * t:384 * t + 384].indirect(T.slotoff[:, 8 * hf:8 * hf + 8]),
-                            T.acol[:, S * t + 128 * hf:S * t + 128 * hf + 128], A.add).then_inc(sem["vh%d" % hf], 1)
-        V.wait_ge(sem["vh%d" % hf], 4)
-        V.quantize_mx(T.mq[:, 128 * hf:128 * hf + 128], T.mqs[:, 128 * hf:128 * hf + 128],
-                      T.h[:, 512 * hf:512 * hf + 512]).then_inc(sem["m%d" % hf], 1)
-        g.wait_ge(sem["m%d" % hf], 1)
-        a, b = 128 * hf, 128 * hf + 128
-        fused([write(offn, off, u8(T.mq[:, a:b]), u8(T.offq[:, a:b]), sem.moff),
-               write(mate, on, u8(T.mq[:, a:b]), u8(T.onq[:, a:b]), sem.mon)])
-    fused([write(offn, off, T.mqs[:], T.offqs[:], sem.moff), write(mate, on, T.mqs[:], T.onqs[:], sem.mon)])
+            bank = T["ps%d" % (4 * (j % 2) + b)]
+            PE.matmul_mx(bank[:, 0:128], T.eq[:, 128 * b:128 * b + 128], T.eqs[:, 128 * b:128 * b + 128],
+                         T[name][:, a:a + 128], T[name + "s"][:, a:a + 128], True, True).then_inc(sem["mm%s%d" % (c, b)], 1)
+            if c in "ab":
+                V.wait_ge(sem["own%d%d" % (1 if c == "a" else 2, b)], 1)
+            V.wait_ge(sem["mm%s%d" % (c, b)], 1)
+            V.tensor_tensor(T.h[:, 4 * hcol[c] + b:4 * (hcol[c] + G):4], bank[:, skip:skip + G],
+                            T.acol[:, W * b + at:W * b + at + G], A.add).then_inc(sem["add" + c], 1)
+        if c == "a":
+            continue
+        k = j
+        end, wide, n = hcol[c] + G, 128, G
+        if c == "g":
+            end, wide, n = 2 * G, 2 * G, 2 * G
+            V.wait_ge(sem.adda, 4)
+        V.wait_ge(sem["add" + c], 4)
+        m = "m%d" % k
+        V.quantize_mx(T[m][:], T[m + "s"][:], T.h[:, 4 * (end - wide):4 * end]).then_inc(sem[m], 1)
+        if c == "g":
+            own_cols("v", 2, 0)
+        g.wait_ge(sem[m], 1)
+        for plane in (False, True):
+            src = piece(m, plane, wide - n, n)
+            fused([write(offn, off, src, piece("offq", plane, end - n, n), sem["loff%d" % k]),
+                   write(mate, on, src, piece("onq", plane, end - n, n), sem["lon%d" % k])])
 
     sec = {prv: 0, r: 1, nxt: 2}
+    who = {"own": r, "on": mate, "off": offn}
+    banks = dict(zip(YS, (0, 1, 4, 2, 3, 5, 6, 7, 0)))
 
     def ycols(q, a, b):
         return slice(S * sec[q] + a, S * sec[q] + b)
 
+    def pick(eng, st, name, tile, a, b):
+        e, cols = (V if eng == "v" else SC), ycols(who[tile], a, b)
+        e.wait_ge(sem.vslot if tile == "own" else sem["lst" + tile], 4 if tile == "own" else len(on if tile == "on" else off))
+        for k in (1, 2, 3):
+            e.wait_ge(sem["c%s%d" % (tile, k)], 1)
+        gather(eng, T.ysb[:, cols], T["y" + tile][:].indirect(T["slot" + tile][:, a // 16:b // 16]), sem["pk" + name])
+        st.wait_ge(sem["pk" + name], 1)
+        st.dma_start(T.y[:, cols], T.ysb[:, cols]).then_inc(sem["st" + name], 16)
+
     PE.wait_ge(sem.vwq, 1)
-    PE.wait_ge(sem.m0, 1)
-    PE.wait_ge(sem.m1, 1)
-    PE.matmul_mx(T.pc0[:, 0:S], T.wq[:], T.wqs[:], T.mq[:], T.mqs[:], True, True).then_inc(sem.mmw, 1)
-    PE.wait_ge(sem.mon, 3 * len(on))
-    PE.matmul_mx(T.pc1[:, 0:S], T.wq[:], T.wqs[:], T.onq[:], T.onqs[:], True, True).then_inc(sem.mmn, 1)
-    PE.wait_ge(sem.moff, 3 * len(off))
-    PE.matmul_mx(T.pc2[:, 0:128], T.wq[:], T.wqs[:], T.offq[:, 0:128], T.offqs[:, 0:128], True, True).then_inc(sem.mmf0, 1)
-    PE.matmul_mx(T.pc3[:, 0:128], T.wq[:], T.wqs[:], T.offq[:, 128:256], T.offqs[:, 128:256], True, True).then_inc(sem.mmf1, 1)
-
-    V.wait_ge(sem.mmw, 1)
-    V.tensor_copy(T.ysb[:, ycols(r, 0, S)], T.pc0[:, 0:S]).then_inc(sem.yw, 1)
-    SC.wait_ge(sem.mmn, 1)
-    SC.activation(T.ysb[:, ycols(mate, 0, S)], T.pc1[:, 0:S], COPY).then_inc(sem.yn, 1)
-    V.wait_ge(sem.mmf0, 1)
-    V.tensor_copy(T.ysb[:, ycols(offn, 0, 128)], T.pc2[:, 0:128]).then_inc(sem.yf0, 1)
-    SC.wait_ge(sem.mmf1, 1)
-    SC.activation(T.ysb[:, ycols(offn, 128, S)], T.pc3[:, 0:128], COPY).then_inc(sem.yf1, 1)
-
-    SY.wait_ge(sem.yw, 1)
-    SY.dma_start(T.y[:, ycols(r, 0, S)], T.ysb[:, ycols(r, 0, S)]).then_inc(sem.stw, 16)
-    SY.wait_ge(sem.yn, 1)
-    SY.dma_start(T.y[:, ycols(mate, 0, S)], T.ysb[:, ycols(mate, 0, S)]).then_inc(sem.stn, 16)
-    SY.wait_ge(sem.yf0, 1)
-    SY.dma_start(T.y[:, ycols(offn, 0, 128)], T.ysb[:, ycols(offn, 0, 128)]).then_inc(sem.stf0, 16)
-    SC.wait_ge(sem.yf1, 1)
-    SC.dma_start(T.y[:, ycols(offn, 128, S)], T.ysb[:, ycols(offn, 128, S)]).then_inc(sem.stf1, 16)
+    PE.wait_ge(sem.m2, 1)
+    for y in YS:
+        tile, k = y[:-1], int(y[-1])
+        at, n = pieces(who[tile])[k - 1]
+        wide = max(n, 128)
+        end = G * (k + 1)
+        if tile == "own":
+            PE.wait_ge(sem["m%d" % k], 1)
+            codes, scales = T["m%d" % k][:], T["m%ds" % k][:]
+        else:
+            PE.wait_ge(sem["l" + y], 2 * len(on if tile == "on" else off))
+            codes, scales = T[tile + "q"][:, end - wide:end], T[tile + "qs"][:, end - wide:end]
+        if y == "off3":
+            PE.wait_ge(sem.cown1, 1)
+        bank = T["ps%d" % banks[y]]
+        PE.matmul_mx(bank[:, 0:wide], T.wq[:], T.wqs[:], codes, scales, True, True).then_inc(sem["y" + y], 1)
+        eng = "v" if tile == "own" else "s"
+        (V if eng == "v" else SC).wait_ge(sem["y" + y], 1)
+        gather(eng, T["y" + tile][:, at:at + n], bank[:, wide - n:wide], sem["c" + y])
+        if y == "own3":
+            pick("v", SY, "own", "own", 0, S)
+        if y == "on3":
+            pick("v", SY, "on", "on", 0, S)
+    pick("v", SY, "offa", "off", 0, 128)
+    pick("s", SC, "offb", "off", 128, S)
 
     g.wait_ge(sem.loc, sent[0])
-    SY.wait_ge(sem.stw, 16)
-    SY.wait_ge(sem.stn, 16)
-    SY.wait_ge(sem.stf0, 16)
-    SC.wait_ge(sem.stf1, 16)
+    for name in PICKS:
+        (SC if name == "offb" else SY).wait_ge(sem["st" + name], 16)

@@ -7,9 +7,6 @@ SCRATCH = {
     "slotr": ("sbuf", [128, 16], "int32"),
     "req": ("sbuf", [128, 24], "uint16"),
     "selfoff": ("sbuf", [128, 4], "uint16"),
-    "la": ("sbuf", [128, 8], "uint16"),
-    "lb": ("sbuf", [128, 16], "uint16"),
-    "lp": ("sbuf", [128, 8], "uint16"),
     "slotown": ("sbuf", [128, 16], "uint16"),
     "sloton": ("sbuf", [128, 16], "uint16"),
     "slotoff": ("sbuf", [128, 16], "uint16"),
@@ -18,69 +15,52 @@ SCRATCH = {
     "s24": ("sbuf", [128, 16], "int32"),
     "place": ("sbuf", [128, 32], "float32"),
     "placet": ("sbuf", [128, 32], "float32"),
-    "placeu": ("sbuf", [128, 16], "uint16"),
-    "ownrow": ("sbuf", [128, 256], "int32"),
-    "invrow": ("sbuf", [128, 384], "int32"),
-    "invw": ("sbuf", [128, 24], "int32"),
+    "placeu": ("sbuf", [128, 8], "uint16"),
+    "ownrow": ("sbuf", [128, 128], "int32"),
+    "invs": ("sbuf", [128, 24], "float32"),
+    "invrow": ("sbuf", [128, 384], "float32"),
+    "invw": ("sbuf", [128, 24], "float32"),
     "inv": ("sbuf", [128, 24], "uint16"),
     "xs": ("sbuf", [128, 2048], "bfloat16"),
     "ws": ("sbuf", [128, 512], "bfloat16"),
-    "ha": ("sbuf", [128, 512], "bfloat16"),
-    "hb": ("sbuf", [128, 768], "bfloat16"),
-    "hp": ("sbuf", [128, 512], "bfloat16"),
-    "f1": ("sbuf", [128, 224], CODE),
-    "f1s": ("sbuf", [128, 224], "uint8"),
-    "f2": ("sbuf", [128, 336], CODE),
-    "f2s": ("sbuf", [128, 336], "uint8"),
-    "f3": ("sbuf", [128, 224], CODE),
-    "f3s": ("sbuf", [128, 224], "uint8"),
+    "ask": ("sbuf", [128, 1664], "bfloat16"),
     "diff": ("sbuf", [128, 128], "int32"),
     "ez": ("sbuf", [128, 520], "bfloat16"),
-    "eq": ("sbuf", [128, 512], CODE),
-    "eqs": ("sbuf", [128, 512], "uint8"),
-    "wq": ("sbuf", [128, 128], CODE),
-    "wqs": ("sbuf", [128, 128], "uint8"),
     "acol": ("sbuf", [128, 1536], "bfloat16"),
-    "h": ("sbuf", [128, 1536], "bfloat16"),
-    "m1": ("sbuf", [128, 192], CODE),
-    "m1s": ("sbuf", [128, 192], "uint8"),
-    "m2": ("sbuf", [128, 128], CODE),
-    "m2s": ("sbuf", [128, 128], "uint8"),
-    "m3": ("sbuf", [128, 128], CODE),
-    "m3s": ("sbuf", [128, 128], "uint8"),
-    "onq": ("sbuf", [128, 384], CODE),
-    "onqs": ("sbuf", [128, 384], "uint8"),
-    "offq": ("sbuf", [128, 384], CODE),
-    "offqs": ("sbuf", [128, 384], "uint8"),
+    "h": ("sbuf", [128, 1664], "bfloat16"),
     "yown": ("sbuf", [128, 384], "float32"),
     "yon": ("sbuf", [128, 384], "float32"),
     "yoff": ("sbuf", [128, 384], "float32"),
     "ysb": ("sbuf", [128, 768], "float32"),
 }
+for _n, _w in (("f0", 224), ("f1", 192), ("f2", 224), ("f3", 224), ("eq", 512), ("wq", 128), ("mg", 128), ("ma", 128),
+               ("mb", 128), ("mp", 128), ("onq", 384), ("offq", 384)):
+    SCRATCH[_n] = ("sbuf", [128, _w], CODE)
+    SCRATCH[_n + "s"] = ("sbuf", [128, _w], "uint8")
+for _i in range(4):
+    SCRATCH["l%d" % _i] = ("sbuf", [128, 8], "uint16")
 for _i in range(8):
     SCRATCH["ps%d" % _i] = ("psum", [128, 512], "float32")
 
-GROUPS = "agbp"
-YS = ("own1", "own2", "own3", "on1", "off1", "on2", "off2", "on3", "off3")
-PICKS = ("own", "on", "offa", "offb")
-SEMAPHORES = (["ldwant", "ldx", "ldw", "ldown", "ldslot", "ldinv", "iota", "iota0", "zero", "vreq", "vself", "ve", "veq", "vwq",
-               "vslot", "k1", "k2", "k3", "k4", "k5", "scat", "vinv", "gself", "lston", "lstoff", "m1", "m2", "m3", "loc"]
-              + [k + c for c in "abp" for k in ("lst", "gv", "gs", "q")]
-              + [k + c for c in GROUPS for k in ("fd", "add")]
-              + ["own%d%d" % (i, t) for i in (1, 2) for t in range(4)]
-              + ["mm%s%d" % (c, b) for c in GROUPS for b in range(4)]
-              + [k + y for y in YS for k in ("l", "y", "c")]
+GROUPS = "gabp"
+YS = ("owng", "owna", "ownb", "ownp", "ona", "onb", "offb", "onp", "offa", "offp")
+PICKS = ("own", "on", "off0", "off1")
+SEMAPHORES = (["ldwant", "ldx", "ldw", "ldown", "ldslot", "ldinv", "iota", "iota0", "zero", "szero", "vreq", "vself", "ve", "veq", "vwq",
+               "vslot", "k1", "k2", "k3", "k4", "k5", "scat", "vsum", "vinv", "gself", "lston", "lstoff", "ownv", "hg", "ha", "lhelp", "loc"]
+              + [k + str(i) for i in range(4) for k in ("lst", "gv", "gs", "q")]
+              + [k + c for c in GROUPS for k in ("fd", "add", "m", "lon", "loff")]
+              + [k + c + str(t) for c in GROUPS for t in range(4) for k in ("ac", "mm")]
+              + [k + y for y in YS for k in ("y", "c")]
               + [k + y for y in PICKS for k in ("pk", "st")])
 
 
 def rank_program(g, core, T, topo):
     r = T.rank_of(core)
-    if r is None:
-        return
     N, CAP, S = 8, 48, 256
     LC = CAP // 16
     G = 2 * CAP
     W = N * CAP
+    PAD = 128 - G
     A, COPY = AluOpType, ActivationFunctionType.Copy
     V, SC, SY, PE, sem = g.vector, g.scalar, g.sync, g.tensor, T.sem
     cores = T.cores
@@ -101,43 +81,29 @@ def rank_program(g, core, T, topo):
                 "b": [s for s in range(N) if chip[s] not in (c, first[c]) and not topo.same_plane(chip[s], c)],
                 "p": [s for s in range(N) if topo.same_plane(chip[s], c)]}
 
-    def pieces(q):
-        gq = groups(q)
-        return [(CAP * min(gq["a"] + gq["g"]), 2 * G), (CAP * gq["b"][0], G), (CAP * gq["p"][0], G)]
-
-    grp = groups(r)
-    mate = [s for s in grp["g"] if s != r][0]
-    prv, nxt = (r - 1) % N, (r + 1) % N
-    offn = prv if nxt == mate else nxt
-    off = topo.engines(core, cores[grp["a"][0]])
-    on = [e for e in topo.engines(core, cores[mate]) if e not in off]
-
     def pos(q):
         return ranks(chip[q]).index(q)
 
-    def lay(q):
-        if pos(q) == 0:
-            return {"tile": 0, "askb": 0, "askm": G, "own": G + CAP, "mate": 2 * G, "landb": 2 * G + CAP,
-                    "wing": (2 * G + CAP - 128, 32), "winb": (2 * G + CAP - 32, 32), "listb": 0, "listm": 2 * LC}
-        return {"landb": 0, "mate": G, "tile": G + CAP, "own": G + CAP, "askm": 2 * G, "askb": 2 * G + CAP,
-                "wing": (G, 0), "winb": (0, 0), "listm": 0, "listb": LC}
+    def far(q):
+        return [s for s in ((q - 1) % N, (q + 1) % N) if chip[s] != chip[q]][0]
 
-    L = lay(r)
+    def helper(q):
+        return [c for c in topo.cores_of(cores[q])
+                if topo.die(c) != topo.die(cores[q]) and topo.may_write(c, cores[far(q)])][pos(q)]
 
     def bits(es):
         return sum(1 << e for e in es)
 
-    def half(i):
-        k = len(off) // 2
-        return off[i * k:(i + 1) * k]
-
     sent = [0]
 
-    def write(d, es, src, dst, rsem):
-        rid, pid = topo.addr(cores[d])[:2]
+    def write_core(c, es, src, dst, rsem):
+        rid, pid = topo.addr(c)[:2]
         sent[0] += len(es)
         return RemoteDMATransfer(dst_ids=[DstId(rid=rid, pnc=pid)], dma_engine_mask=bits(es), remote_sem=rsem,
                                  srcs=[src], dsts=[dst])
+
+    def write(d, es, src, dst, rsem):
+        return write_core(cores[d], es, src, dst, rsem)
 
     def fused(ts):
         g.remote_dma_fused(ts, local_sem=sem.loc)
@@ -145,78 +111,122 @@ def rank_program(g, core, T, topo):
     def piece(name, plane, a, n):
         return T[name + "s"][:, a:a + n] if plane else T[name][:, a:a + n].bitcast(dt.uint8)
 
+    if r is None:
+        for q in range(N):
+            if helper(q) == core:
+                es = topo.engines(core, cores[far(q)])
+                n = len([e for e in topo.engines(cores[q], core) if e not in es])
+                g.wait_ge(sem.lston, n // 2)
+                fused([write(far(q), es, T.slotoff[:], T.slotoff[:], sem.lstoff)])
+                for s, a, k in ((sem.hg, 0, G), (sem.ha, G, CAP)):
+                    g.wait_ge(s, 2 * n)
+                    for plane in (False, True):
+                        fused([write(far(q), es, piece("offq", plane, a, k), piece("offq", plane, a, k), sem.lhelp)])
+                g.wait_ge(sem.loc, sent[0])
+        return
+
+    grp = groups(r)
+    mate = [s for s in grp["g"] if s != r][0]
+    prv, nxt = (r - 1) % N, (r + 1) % N
+    offn = far(r)
+    off = topo.engines(core, cores[offn])
+    on = [e for e in topo.engines(core, cores[mate]) if e not in off]
+    like, unlike = grp["a"][pos(r)], grp["a"][1 - pos(r)]
+
+    def half(i, es=off):
+        k = len(es) // 2
+        return es[i * k:(i + 1) * k]
+
+    names = [("p", G), ("b", G), ("unlike", CAP), ("mate", CAP), ("own", CAP), ("pad", PAD), ("like", CAP)]
+    if pos(r) == 1:
+        names = names[::-1]
+    col, a = {}, 0
+    for k, n in names:
+        col[k], a = a, a + n
+    fwd = pos(r) == 0
+    tiles = [(min(col["own"], col["like"]), 128), (min(col["own"], col["unlike"]), 3 * CAP),
+             (col["b"] - (0 if fwd else PAD), 128), (col["p"] - (0 if fwd else PAD), 128)]
+    t1 = 0 if fwd else CAP
+
+    def mate_at(q):
+        return 3 * CAP if pos(q) == 0 else 0
+
     for k, q in enumerate((SY, SC)):
         q.dma_start(T.wantr[16 * k:16 * k + 16, :], T.want[:]).then_inc(sem.ldwant, 16)
         q.dma_start(T.slotr[16 * k:16 * k + 16, :], T.slot[:]).then_inc(sem.ldslot, 16)
-    SY.dma_start(T.xs[:], T.x[:]).then_inc(sem.ldx, 16)
+    V.memset(T.ownrow[:], 0).then_inc(sem.iota0, 1)
     SC.wait_ge(sem.iota0, 1)
     SY.wait_ge(sem.iota0, 1)
-    for k, q in enumerate((SC, SC, SY, SC)):
-        q.dma_start(T.ownrow[16 * k:16 * k + 1, :], T.own[:]).then_inc(sem.ldown, 16)
+    for k, q in enumerate((SC, SY, SC, SC)):
+        q.dma_start(T.ownrow[16 * k:128:64, :], T.own[:]).then_inc(sem.ldown, 16)
+    SY.dma_start(T.xs[:], T.x[:]).then_inc(sem.ldx, 16)
     SY.dma_start(T.ws[:], T.w[:]).then_inc(sem.ldw, 16)
+    zeros = T.ask[:, 4 * col["pad"]:4 * (col["pad"] + PAD)]
+    SC.wait_ge(sem.zero, 3)
+    for k in range(W // 128):
+        SC.activation(T.invrow[:, 128 * k:128 * k + 128], zeros, COPY).then_inc(sem.szero, 1)
     blocks = [slice(32 * k, 32 * k + 32) for k in range(4)]
 
     def make_e(b):
         V.quantize_mx(T.eq[:, 128 * b:128 * b + 128], T.eqs[:, 128 * b:128 * b + 128],
                       T.ez[:, 3 - b:515 - b]).then_inc(sem.veq, 1)
 
-    g.iota(T.ownrow[:], [[0, S]], 0, 0).then_inc(sem.iota0, 1)
     g.iota(T.diff[:], [[1, 128]], 0, -1).then_inc(sem.iota, 1)
     V.memset(T.ez[:], 0.0).then_inc(sem.zero, 1)
-    V.memset(T.ha[:, 4 * G:512], 0.0).then_inc(sem.zero, 1)
-    V.memset(T.hp[:, 4 * G:512], 0.0).then_inc(sem.zero, 1)
-    V.memset(T.invrow[:], 0).then_inc(sem.zero, 1)
+    V.memset(zeros, 0.0).then_inc(sem.zero, 1)
+    V.memset(T.h[:, 0:4 * PAD], 0.0).then_inc(sem.zero, 1)
+    V.wait_ge(sem.iota, 1)
+    V.wait_ge(sem.zero, 3)
+    V.tensor_scalar(T.ez[:, 3:515:4], T.diff[:], 0, 0.5, A.is_equal, A.mult).then_inc(sem.ve, 1)
     V.wait_ge(sem.ldwant, 32)
     for b in blocks:
         V.tensor_scalar(T.req[b, :], T.wantr[0:32, :], 4, 0, A.mult, A.max).then_inc(sem.vreq, 1)
-    V.wait_ge(sem.iota, 1)
-    V.wait_ge(sem.zero, 4)
-    V.tensor_scalar(T.ez[:, 3:515:4], T.diff[:], 0, 0.5, A.is_equal, A.mult).then_inc(sem.ve, 1)
-    V.wait_ge(sem.vreq, 4)
-    V.tensor_copy(T.selfoff[:, 0:LC], T.req[:, LC * r:LC * r + LC]).then_inc(sem.vself, 1)
-    V.wait_ge(sem.ve, 1)
 
     b0 = blocks[0]
     V.wait_ge(sem.ldslot, 32)
     V.tensor_scalar(T.hi[b0, :], T.slotr[b0, :], 4, None, A.arith_shift_right).then_inc(sem.k1, 1)
     V.tensor_scalar(T.s24[b0, :], T.slotr[b0, :], W // 16, None, A.mult).then_inc(sem.k2, 1)
+    V.wait_ge(sem.vreq, 4)
+    V.tensor_copy(T.selfoff[:, 0:LC], T.req[:, LC * r:LC * r + LC]).then_inc(sem.vself, 1)
     V.wait_ge(sem.k1, 1)
     V.tensor_scalar(T.hi2[b0, :], T.hi[b0, :], 1 - W, None, A.mult).then_inc(sem.k2, 1)
-    make_e(0)
+    V.tensor_copy(T.slotown[b0, :], T.slotr[b0, :]).then_inc(sem.vslot, 1)
     V.wait_ge(sem.k2, 2)
     for k in range(2):
         V.tensor_tensor(T.place[b0, 16 * k:16 * k + 16], T.s24[b0, :], T.hi2[b0, :], A.add).then_inc(sem.k3, 1)
+    V.tensor_copy(T.slotown[blocks[1], :], T.slotr[b0, :]).then_inc(sem.vslot, 1)
     V.wait_ge(sem.k3, 2)
     V.transpose(T.placet[b0, :], T.place[b0, :]).then_inc(sem.k4, 1)
-    make_e(1)
+    V.tensor_copy(T.slotown[blocks[2], :], T.slotr[b0, :]).then_inc(sem.vslot, 1)
     V.wait_ge(sem.k4, 1)
-    for b in blocks:
-        V.tensor_copy(T.placeu[b, :], T.placet[b0, 0:16]).then_inc(sem.k5, 1)
+    for k, b in enumerate(blocks):
+        V.tensor_copy(T.placeu[b, :], T.placet[b0, 8 * (k // 2):8 * (k // 2) + 8]).then_inc(sem.k5, 1)
+    V.tensor_copy(T.slotown[blocks[3], :], T.slotr[b0, :]).then_inc(sem.vslot, 1)
     V.wait_ge(sem.k5, 4)
     V.wait_ge(sem.ldown, 64)
+    V.wait_ge(sem.szero, 3)
     V.tensor_copy(T.invrow[:].indirect(T.placeu[:]), T.ownrow[:]).then_inc(sem.scat, 1)
     SY.wait_ge(sem.scat, 1)
-    SY.dma_start(T.invw[0:64, :], T.invrow[0:64:16, :]).then_inc(sem.ldinv, 16)
-    for b in blocks:
-        V.tensor_copy(T.slotown[b, :], T.slotr[b0, :]).then_inc(sem.vslot, 1)
-    make_e(2)
-    make_e(3)
+    SY.dma_start(T.invw[:], T.invrow[0:128:16, :]).then_inc(sem.ldinv, 16)
+    V.wait_ge(sem.ve, 1)
+    for b in range(4):
+        make_e(b)
 
-    def reqs(q):
-        return T.req[:, LC * q:LC * q + LC]
+    asks = [[like], [unlike, mate] if fwd else [mate, unlike], grp["b"], grp["p"]]
+
+    def engines(i, q):
+        return on if q == mate else off if i < 2 else half(asks[i].index(q))
 
     g.wait_ge(sem.vreq, 4)
-    for c in "abp":
+    for i in range(4):
         ts = []
-        for i, q in enumerate(grp[c]):
-            k = LC * pos(r) + (lay(q)["listb"] if c == "b" else 0)
-            ts.append(write(q, half(i), reqs(q), T["l" + c][:, k:k + LC], sem["lst" + c]))
-        if c == "b":
-            k = lay(mate)["listm"]
-            ts.append(write(mate, on, reqs(mate), T.lb[:, k:k + LC], sem.lstb))
+        for q in asks[i]:
+            k = 0 if i == 0 else pos(r) if i > 1 else (1 - pos(q) if q == mate else pos(q))
+            ts.append(write(q, engines(i, q), T.req[:, LC * q:LC * q + LC], T["l%d" % i][:, LC * k:LC * k + LC], sem["lst%d" % i]))
         fused(ts)
     g.wait_ge(sem.vslot, 4)
-    fused([write(offn, off, T.slotown[:], T.slotoff[:], sem.lstoff), write(mate, on, T.slotown[:], T.sloton[:], sem.lston)])
+    fused([write_core(helper(r), half(0, on), T.slotown[:], T.slotoff[:], sem.lston),
+           write(mate, half(1, on), T.slotown[:], T.sloton[:], sem.lston)])
 
     def gather(eng, out, src, s, scale=None):
         if eng == "v":
@@ -232,149 +242,147 @@ def rank_program(g, core, T, topo):
     def xcols(t, offs):
         return T.xs[:, t:2048].indirect(offs)
 
-    pc = pieces(r)
-    halves = {1: pc[0][0], 2: min(pc[1][0], pc[2][0])}
+    def own_cols(eng, a, n, t, s):
+        gather(eng, T.acol[:, W * t + a:W * t + a + n], xcols(t, T.inv[:, a // 16:(a + n) // 16]), s, 0.5)
 
-    def own_cols(eng, i, t):
-        a = halves[i]
-        gather(eng, T.acol[:, W * t + a:W * t + a + 2 * G], xcols(t, T.inv[:, a // 16:(a + 2 * G) // 16]),
-               sem["own%d%d" % (i, t)], 0.5)
-
-    t2 = L["tile"]
-    o2 = 4 * (L["own"] - t2)
-    a2 = 4 * (min(L["askm"], L["askb"]) - t2)
     SC.wait_ge(sem.vself, 1)
     SC.wait_ge(sem.ldx, 16)
     for t in range(4):
-        gather("s", T.hb[:, o2 + t:o2 + 4 * CAP:4], xcols(t, T.selfoff[:, 0:LC]), sem.gself)
+        gather("s", T.ask[:, 4 * col["own"] + t:4 * (col["own"] + CAP):4], xcols(t, T.selfoff[:, 0:LC]), sem.gself)
     V.wait_ge(sem.ldx, 16)
+    V.wait_ge(sem.gself, 4)
+    starts = [col["like"], min(col["unlike"], col["mate"]), col["b"], col["p"]]
     for eng, q in (("v", V), ("s", SC)):
-        for c in "abp":
-            q.wait_ge(sem["lst" + c], len(off) + (len(on) if c == "b" else 0))
+        for i in range(4):
+            n = len(asks[i])
+            q.wait_ge(sem["lst%d" % i], sum(len(engines(i, s)) for s in asks[i]))
             for t in ((0, 1) if eng == "v" else (2, 3)):
-                if c == "b":
-                    gather(eng, T.hb[:, a2 + t:a2 + 4 * (G + CAP):4], xcols(t, T.lb[:, 0:3 * LC]), sem["g" + eng + c])
-                else:
-                    gather(eng, T["h" + c][:, t:4 * G:4], xcols(t, T["l" + c][:, 0:2 * LC]), sem["g" + eng + c])
+                gather(eng, T.ask[:, 4 * starts[i] + t:4 * (starts[i] + n * CAP):4], xcols(t, T["l%d" % i][:, 0:n * LC]),
+                       sem["g%s%d" % (eng, i)])
             if eng == "v":
-                V.wait_ge(sem["gv" + c], 2)
-                V.wait_ge(sem["gs" + c], 2)
-                if c == "b":
-                    V.wait_ge(sem.gself, 4)
-                    V.quantize_mx(T.f2[:, t2:t2 + 2 * G], T.f2s[:, t2:t2 + 2 * G], T.hb[:]).then_inc(sem.qb, 1)
-                else:
-                    f = "f1" if c == "a" else "f3"
-                    V.quantize_mx(T[f][:, 0:128], T[f + "s"][:, 0:128], T["h" + c][:]).then_inc(sem["q" + c], 1)
-    V.wait_ge(sem.ldinv, 16)
-    for k in range(2):
-        V.tensor_scalar(T.inv[64 * k:64 * k + 64, :], T.invw[0:64, :], 4, None, A.mult).then_inc(sem.vinv, 1)
-    V.wait_ge(sem.ldw, 16)
-    V.quantize_mx(T.wq[:], T.wqs[:], T.ws[:]).then_inc(sem.vwq, 1)
+                V.wait_ge(sem["gv%d" % i], 2)
+                V.wait_ge(sem["gs%d" % i], 2)
+                a, wide = tiles[i]
+                o = t1 if i == 1 else 0
+                V.quantize_mx(T["f%d" % i][:, o:o + wide], T["f%ds" % i][:, o:o + wide],
+                              T.ask[:, 4 * a:4 * (a + wide)]).then_inc(sem["q%d" % i], 1)
+                if i == 2:
+                    V.wait_ge(sem.ldinv, 16)
+                    V.tensor_tensor(T.invs[0:64, :], T.invw[0:64, :], T.invw[64:128, :], A.add).then_inc(sem.vsum, 1)
+                    V.wait_ge(sem.vsum, 1)
+                    for k in range(2):
+                        V.tensor_scalar(T.inv[64 * k:64 * k + 64, :], T.invs[0:64, :], 4, None, A.mult).then_inc(sem.vinv, 1)
+    slot0 = {c: CAP * grp[c][0] for c in GROUPS}
     V.wait_ge(sem.vinv, 2)
-    own_cols("v", 1, 0)
+    own_cols("v", min(slot0["b"], slot0["p"]), 2 * G, 0, sem.ownv)
     SC.wait_ge(sem.vinv, 2)
-    for i in (1, 2):
-        for t in (1, 2, 3):
-            own_cols("s", i, t)
+    for c in GROUPS:
+        for t in range(0 if c in "ga" else 1, 4):
+            own_cols("s", slot0[c], G, t, sem["ac%s%d" % (c, t)])
 
-    for c in "abp":
-        g.wait_ge(sem["q" + c], 1)
+    for i in range(4):
+        g.wait_ge(sem["q%d" % i], 1)
         for plane in (False, True):
             ts = []
-            for i, q in enumerate(grp[c]):
-                if c == "b":
-                    src = piece("f2", plane, L["askb"] + CAP * i, CAP)
-                    dst = piece("f2", plane, lay(q)["landb"] + CAP * pos(r), CAP)
+            for k, q in enumerate(asks[i]):
+                src = piece("f%d" % i, plane, starts[i] - tiles[i][0] + (t1 if i == 1 else 0) + CAP * k, CAP)
+                if q == mate:
+                    dst, s = piece("f1", plane, mate_at(q), CAP), sem.fdg
                 else:
-                    f = "f1" if c == "a" else "f3"
-                    src, dst = piece(f, plane, CAP * i, CAP), piece(f, plane, 128 + CAP * pos(r), CAP)
-                ts.append(write(q, half(i), src, dst, sem["fd" + c]))
-            if c == "b":
-                ts.append(write(mate, on, piece("f2", plane, L["askm"], CAP),
-                                piece("f2", plane, lay(mate)["mate"], CAP), sem.fdg))
+                    dst, s = piece("f%d" % (i if i > 1 else 0), plane, 128 + CAP * pos(r), CAP), sem["fd" + "aabp"[i]]
+                ts.append(write(q, engines(i, q), src, dst, s))
             fused(ts)
 
-    win = {"a": ("f1", G, 32), "g": ("f2",) + L["wing"], "b": ("f2",) + L["winb"], "p": ("f3", G, 32)}
-    hcol = {"a": CAP * grp["a"][0] - pc[0][0], "g": CAP * grp["g"][0] - pc[0][0], "b": 2 * G, "p": 3 * G}
+    win = {"g": ("f1", 4 * CAP - 128, PAD) if fwd else ("f1", 0, 0), "a": ("f0", G, PAD), "b": ("f2", G, PAD), "p": ("f3", G, PAD)}
     PE.wait_ge(sem.veq, 4)
     for j, c in enumerate(GROUPS):
         name, a, skip = win[c]
-        if c != "b":
-            PE.wait_ge(sem["q" + {"a": "a", "g": "b", "p": "p"}[c]], 1)
-        PE.wait_ge(sem["fd" + c], 2 * len(on if c == "g" else off))
+        PE.wait_ge(sem["q" + name[1]], 1)
+        PE.wait_ge(sem["fd" + c], {"g": 2 * len(on), "a": 4 * len(off)}.get(c, 2 * len(off)))
         if j >= 2:
             PE.wait_ge(sem["add" + GROUPS[j - 2]], 4)
-        at = CAP * grp[c][0]
+        hc = PAD + G * j
         for b in range(4):
             bank = T["ps%d" % (4 * (j % 2) + b)]
             PE.matmul_mx(bank[:, 0:128], T.eq[:, 128 * b:128 * b + 128], T.eqs[:, 128 * b:128 * b + 128],
                          T[name][:, a:a + 128], T[name + "s"][:, a:a + 128], True, True).then_inc(sem["mm%s%d" % (c, b)], 1)
-            if c in "ab":
-                V.wait_ge(sem["own%d%d" % (1 if c == "a" else 2, b)], 1)
+            if c in "bp" and b == 0:
+                V.wait_ge(sem.ownv, 1)
+            else:
+                V.wait_ge(sem["ac%s%d" % (c, b)], 1)
             V.wait_ge(sem["mm%s%d" % (c, b)], 1)
-            V.tensor_tensor(T.h[:, 4 * hcol[c] + b:4 * (hcol[c] + G):4], bank[:, skip:skip + G],
-                            T.acol[:, W * b + at:W * b + at + G], A.add).then_inc(sem["add" + c], 1)
-        if c == "a":
-            continue
-        k = j
-        end, wide, n = hcol[c] + G, 128, G
-        if c == "g":
-            end, wide, n = 2 * G, 2 * G, 2 * G
-            V.wait_ge(sem.adda, 4)
+            V.tensor_tensor(T.h[:, 4 * hc + b:4 * (hc + G):4], bank[:, skip:skip + G],
+                            T.acol[:, W * b + slot0[c]:W * b + slot0[c] + G], A.add).then_inc(sem["add" + c], 1)
         V.wait_ge(sem["add" + c], 4)
-        m = "m%d" % k
-        V.quantize_mx(T[m][:], T[m + "s"][:], T.h[:, 4 * (end - wide):4 * end]).then_inc(sem[m], 1)
-        if c == "g":
-            own_cols("v", 2, 0)
+        m = "m" + c
+        V.quantize_mx(T[m][:], T[m + "s"][:], T.h[:, 4 * (hc - PAD):4 * (hc + G)]).then_inc(sem[m], 1)
         g.wait_ge(sem[m], 1)
+        at = G * j
+        if c in "ga":
+            for plane in (False, True):
+                n = G if c == "g" else CAP
+                ts = [write_core(helper(r), on, piece(m, plane, PAD, n), piece("offq", plane, at, n), sem["h" + c])]
+                if c == "a":
+                    ts.append(write(offn, off, piece(m, plane, PAD + n, n), piece("offq", plane, at + n, n), sem.loffa))
+                fused(ts)
         for plane in (False, True):
-            src = piece(m, plane, wide - n, n)
-            fused([write(offn, off, src, piece("offq", plane, end - n, n), sem["loff%d" % k]),
-                   write(mate, on, src, piece("onq", plane, end - n, n), sem["lon%d" % k])])
+            src = piece(m, plane, PAD, G)
+            ts = [write(mate, on, src, piece("onq", plane, at, G), sem["lon" + c])]
+            if c in "bp":
+                ts.append(write(offn, off, src, piece("offq", plane, at, G), sem["loff" + c]))
+            fused(ts)
 
     sec = {prv: 0, r: 1, nxt: 2}
     who = {"own": r, "on": mate, "off": offn}
-    banks = dict(zip(YS, (0, 1, 4, 2, 3, 5, 6, 7, 0)))
+    landed = {"ona": (("long", 2), ("lona", 2)), "offb": (("loffa", 2), ("loffb", 2)), "offa": (("lhelp", 4),)}
 
     def ycols(q, a, b):
         return slice(S * sec[q] + a, S * sec[q] + b)
 
+    def parts(y):
+        return "ga" if y in ("ona", "offa") else y[-1]
+
     def pick(eng, st, name, tile, a, b):
         e, cols = (V if eng == "v" else SC), ycols(who[tile], a, b)
-        e.wait_ge(sem.vslot if tile == "own" else sem["lst" + tile], 4 if tile == "own" else len(on if tile == "on" else off))
-        for k in (1, 2, 3):
-            e.wait_ge(sem["c%s%d" % (tile, k)], 1)
+        e.wait_ge(sem.vslot if tile == "own" else sem["lst" + tile], {"own": 4, "on": len(on) // 2, "off": len(off)}[tile])
+        for y in YS:
+            if y[:-1] == tile:
+                e.wait_ge(sem["c" + y], len(parts(y)))
         gather(eng, T.ysb[:, cols], T["y" + tile][:].indirect(T["slot" + tile][:, a // 16:b // 16]), sem["pk" + name])
         st.wait_ge(sem["pk" + name], 1)
         st.dma_start(T.y[:, cols], T.ysb[:, cols]).then_inc(sem["st" + name], 16)
 
+    V.wait_ge(sem.ldw, 16)
+    V.quantize_mx(T.wq[:], T.wqs[:], T.ws[:]).then_inc(sem.vwq, 1)
     PE.wait_ge(sem.vwq, 1)
-    PE.wait_ge(sem.m2, 1)
-    for y in YS:
-        tile, k = y[:-1], int(y[-1])
-        at, n = pieces(who[tile])[k - 1]
-        wide = max(n, 128)
-        end = G * (k + 1)
+    PE.wait_ge(sem.mp, 1)
+    for j, y in enumerate(YS):
+        tile, c = y[:-1], y[-1]
+        wide = max(G * len(parts(y)), 128)
+        end = G * (GROUPS.index(c) + 1)
         if tile == "own":
-            PE.wait_ge(sem["m%d" % k], 1)
-            codes, scales = T["m%d" % k][:], T["m%ds" % k][:]
+            PE.wait_ge(sem["m" + c], 1)
+            codes, scales = T["m" + c][:], T["m" + c + "s"][:]
         else:
-            PE.wait_ge(sem["l" + y], 2 * len(on if tile == "on" else off))
+            for s, n in landed.get(y, (("l" + y, 2),)):
+                PE.wait_ge(sem[s], n * len(on if tile == "on" else off))
             codes, scales = T[tile + "q"][:, end - wide:end], T[tile + "qs"][:, end - wide:end]
-        if y == "off3":
-            PE.wait_ge(sem.cown1, 1)
-        bank = T["ps%d" % banks[y]]
+        if j >= 8:
+            PE.wait_ge(sem["c" + YS[j - 8]], 1)
+        bank = T["ps%d" % (j % 8)]
         PE.matmul_mx(bank[:, 0:wide], T.wq[:], T.wqs[:], codes, scales, True, True).then_inc(sem["y" + y], 1)
         eng = "v" if tile == "own" else "s"
         (V if eng == "v" else SC).wait_ge(sem["y" + y], 1)
-        gather(eng, T["y" + tile][:, at:at + n], bank[:, wide - n:wide], sem["c" + y])
-        if y == "own3":
+        for k, p in enumerate(reversed(parts(y))):
+            at = CAP * groups(who[tile])[p][0]
+            gather(eng, T["y" + tile][:, at:at + G], bank[:, wide - G * (k + 1):wide - G * k], sem["c" + y])
+        if y == "ownp":
             pick("v", SY, "own", "own", 0, S)
-        if y == "on3":
+        if y == "onp":
             pick("v", SY, "on", "on", 0, S)
-    pick("v", SY, "offa", "off", 0, 128)
-    pick("s", SC, "offb", "off", 128, S)
+    pick("v", SY, "off0", "off", 0, 128)
+    pick("s", SC, "off1", "off", 128, S)
 
     g.wait_ge(sem.loc, sent[0])
     for name in PICKS:
-        (SC if name == "offb" else SY).wait_ge(sem["st" + name], 16)
+        (SC if name == "off1" else SY).wait_ge(sem["st" + name], 16)

from concourse.bass import DstId, RemoteDMATransfer
from concourse.mybir import dt, AluOpType, ActivationFunctionType

CODE = "float8_e4m3fn_x4"
SCRATCH = {
    "wantr": ("sbuf", [128, 24], "int32"),
    "slotr": ("sbuf", [128, 16], "int32"),
    "req": ("sbuf", [128, 24], "uint16"),
    "selfoff": ("sbuf", [128, 4], "uint16"),
    "slotown": ("sbuf", [128, 16], "uint16"),
    "sloton": ("sbuf", [128, 16], "uint16"),
    "slotoff": ("sbuf", [128, 16], "uint16"),
    "hi": ("sbuf", [128, 16], "int32"),
    "hi2": ("sbuf", [128, 16], "int32"),
    "s24": ("sbuf", [128, 16], "int32"),
    "place": ("sbuf", [128, 32], "float32"),
    "placet": ("sbuf", [128, 32], "float32"),
    "placeu": ("sbuf", [128, 8], "uint16"),
    "ownrow": ("sbuf", [128, 128], "int32"),
    "invs": ("sbuf", [128, 24], "float32"),
    "invrow": ("sbuf", [128, 384], "float32"),
    "invw": ("sbuf", [128, 24], "float32"),
    "inv": ("sbuf", [128, 24], "uint16"),
    "xs": ("sbuf", [128, 2048], "bfloat16"),
    "ws": ("sbuf", [128, 512], "bfloat16"),
    "ask": ("sbuf", [128, 1664], "bfloat16"),
    "diff": ("sbuf", [128, 128], "int32"),
    "ez": ("sbuf", [128, 520], "bfloat16"),
    "acol": ("sbuf", [128, 1536], "bfloat16"),
    "h": ("sbuf", [128, 1664], "bfloat16"),
    "yown": ("sbuf", [128, 384], "float32"),
    "yon": ("sbuf", [128, 384], "float32"),
    "yoff": ("sbuf", [128, 384], "float32"),
    "ysb": ("sbuf", [128, 768], "float32"),
}
for _n, _w in (("f0", 224), ("f1", 192), ("f2", 224), ("f3", 224), ("eq", 512), ("wq", 128), ("mg", 128), ("ma", 128),
               ("mb", 128), ("mp", 128), ("onq", 384), ("offq", 384)):
    SCRATCH[_n] = ("sbuf", [128, _w], CODE)
    SCRATCH[_n + "s"] = ("sbuf", [128, _w], "uint8")
for _i in range(4):
    SCRATCH["l%d" % _i] = ("sbuf", [128, 8], "uint16")
for _i in range(8):
    SCRATCH["ps%d" % _i] = ("psum", [128, 512], "float32")

GROUPS = "gabp"
YS = ("owng", "owna", "ownb", "ownp", "ona", "onb", "offb", "onp", "offa", "offp")
PICKS = ("own", "on", "off0", "off1")
SEMAPHORES = (["ldwant", "ldx", "ldw", "ldown", "ldslot", "ldinv", "iota", "iota0", "zero", "szero", "vreq", "vself", "ve", "veq", "vwq",
               "vslot", "k1", "k2", "k3", "k4", "k5", "scat", "vsum", "vinv", "gself", "lston", "lstoff", "ownv", "hg", "ha", "lhelp", "loc"]
              + [k + str(i) for i in range(4) for k in ("lst", "gv", "gs", "q")]
              + [k + c for c in GROUPS for k in ("fd", "add", "m", "lon", "loff")]
              + [k + c + str(t) for c in GROUPS for t in range(4) for k in ("ac", "mm")]
              + [k + y for y in YS for k in ("y", "c")]
              + [k + y for y in PICKS for k in ("pk", "st")])


def rank_program(g, core, T, topo):
    r = T.rank_of(core)
    N, CAP, S = 8, 48, 256
    LC = CAP // 16
    G = 2 * CAP
    W = N * CAP
    PAD = 128 - G
    A, COPY = AluOpType, ActivationFunctionType.Copy
    V, SC, SY, PE, sem = g.vector, g.scalar, g.sync, g.tensor, T.sem
    cores = T.cores
    chip = [topo.chip(c) for c in cores]
    chips = sorted(set(chip), key=chip.index)
    first = {}
    for c in chips:
        if c not in first:
            d = [d for d in chips if d != c and d not in first and not topo.same_plane(c, d)][0]
            first[c], first[d] = d, c

    def ranks(c):
        return [s for s in range(N) if chip[s] == c]

    def groups(q):
        c = chip[q]
        return {"a": ranks(first[c]), "g": ranks(c),
                "b": [s for s in range(N) if chip[s] not in (c, first[c]) and not topo.same_plane(chip[s], c)],
                "p": [s for s in range(N) if topo.same_plane(chip[s], c)]}

    def pos(q):
        return ranks(chip[q]).index(q)

    def far(q):
        return [s for s in ((q - 1) % N, (q + 1) % N) if chip[s] != chip[q]][0]

    def helper(q):
        return [c for c in topo.cores_of(cores[q])
                if topo.die(c) != topo.die(cores[q]) and topo.may_write(c, cores[far(q)])][pos(q)]

    def bits(es):
        return sum(1 << e for e in es)

    sent = [0]

    def write_core(c, es, src, dst, rsem):
        rid, pid = topo.addr(c)[:2]
        sent[0] += len(es)
        return RemoteDMATransfer(dst_ids=[DstId(rid=rid, pnc=pid)], dma_engine_mask=bits(es), remote_sem=rsem,
                                 srcs=[src], dsts=[dst])

    def write(d, es, src, dst, rsem):
        return write_core(cores[d], es, src, dst, rsem)

    def fused(ts):
        g.remote_dma_fused(ts, local_sem=sem.loc)

    def piece(name, plane, a, n):
        return T[name + "s"][:, a:a + n] if plane else T[name][:, a:a + n].bitcast(dt.uint8)

    if r is None:
        for q in range(N):
            if helper(q) == core:
                es = topo.engines(core, cores[far(q)])
                n = len([e for e in topo.engines(cores[q], core) if e not in es])
                g.wait_ge(sem.lston, n // 2)
                fused([write(far(q), es, T.slotoff[:], T.slotoff[:], sem.lstoff)])
                for s, a, k in ((sem.hg, 0, G), (sem.ha, G, CAP)):
                    g.wait_ge(s, 2 * n)
                    for plane in (False, True):
                        fused([write(far(q), es, piece("offq", plane, a, k), piece("offq", plane, a, k), sem.lhelp)])
                g.wait_ge(sem.loc, sent[0])
        return

    grp = groups(r)
    mate = [s for s in grp["g"] if s != r][0]
    prv, nxt = (r - 1) % N, (r + 1) % N
    offn = far(r)
    off = topo.engines(core, cores[offn])
    on = [e for e in topo.engines(core, cores[mate]) if e not in off]
    like, unlike = grp["a"][pos(r)], grp["a"][1 - pos(r)]

    def half(i, es=off):
        k = len(es) // 2
        return es[i * k:(i + 1) * k]

    names = [("p", G), ("b", G), ("unlike", CAP), ("mate", CAP), ("own", CAP), ("pad", PAD), ("like", CAP)]
    if pos(r) == 1:
        names = names[::-1]
    col, a = {}, 0
    for k, n in names:
        col[k], a = a, a + n
    fwd = pos(r) == 0
    tiles = [(min(col["own"], col["like"]), 128), (min(col["own"], col["unlike"]), 3 * CAP),
             (col["b"] - (0 if fwd else PAD), 128), (col["p"] - (0 if fwd else PAD), 128)]
    t1 = 0 if fwd else CAP

    def mate_at(q):
        return 3 * CAP if pos(q) == 0 else 0

    for k, q in enumerate((SY, SC)):
        q.dma_start(T.wantr[16 * k:16 * k + 16, :], T.want[:]).then_inc(sem.ldwant, 16)
        q.dma_start(T.slotr[16 * k:16 * k + 16, :], T.slot[:]).then_inc(sem.ldslot, 16)
    V.memset(T.ownrow[:], 0).then_inc(sem.iota0, 1)
    SC.wait_ge(sem.iota0, 1)
    SY.wait_ge(sem.iota0, 1)
    for k, q in enumerate((SC, SY, SC, SC)):
        q.dma_start(T.ownrow[16 * k:128:64, :], T.own[:]).then_inc(sem.ldown, 16)
    SY.dma_start(T.xs[:], T.x[:]).then_inc(sem.ldx, 16)
    SY.dma_start(T.ws[:], T.w[:]).then_inc(sem.ldw, 16)
    zeros = T.ask[:, 4 * col["pad"]:4 * (col["pad"] + PAD)]
    SC.wait_ge(sem.zero, 3)
    for k in range(W // 128):
        SC.activation(T.invrow[:, 128 * k:128 * k + 128], zeros, COPY).then_inc(sem.szero, 1)
    blocks = [slice(32 * k, 32 * k + 32) for k in range(4)]

    def make_e(b):
        V.quantize_mx(T.eq[:, 128 * b:128 * b + 128], T.eqs[:, 128 * b:128 * b + 128],
                      T.ez[:, 3 - b:515 - b]).then_inc(sem.veq, 1)

    g.iota(T.diff[:], [[1, 128]], 0, -1).then_inc(sem.iota, 1)
    V.memset(T.ez[:], 0.0).then_inc(sem.zero, 1)
    V.memset(zeros, 0.0).then_inc(sem.zero, 1)
    V.memset(T.h[:, 0:4 * PAD], 0.0).then_inc(sem.zero, 1)
    V.wait_ge(sem.iota, 1)
    V.wait_ge(sem.zero, 3)
    V.tensor_scalar(T.ez[:, 3:515:4], T.diff[:], 0, 0.5, A.is_equal, A.mult).then_inc(sem.ve, 1)
    V.wait_ge(sem.ldwant, 32)
    for b in blocks:
        V.tensor_scalar(T.req[b, :], T.wantr[0:32, :], 4, 0, A.mult, A.max).then_inc(sem.vreq, 1)

    b0 = blocks[0]
    V.wait_ge(sem.ldslot, 32)
    V.tensor_scalar(T.hi[b0, :], T.slotr[b0, :], 4, None, A.arith_shift_right).then_inc(sem.k1, 1)
    V.tensor_scalar(T.s24[b0, :], T.slotr[b0, :], W // 16, None, A.mult).then_inc(sem.k2, 1)
    V.wait_ge(sem.vreq, 4)
    V.tensor_copy(T.selfoff[:, 0:LC], T.req[:, LC * r:LC * r + LC]).then_inc(sem.vself, 1)
    V.wait_ge(sem.k1, 1)
    V.tensor_scalar(T.hi2[b0, :], T.hi[b0, :], 1 - W, None, A.mult).then_inc(sem.k2, 1)
    V.tensor_copy(T.slotown[b0, :], T.slotr[b0, :]).then_inc(sem.vslot, 1)
    V.wait_ge(sem.k2, 2)
    for k in range(2):
        V.tensor_tensor(T.place[b0, 16 * k:16 * k + 16], T.s24[b0, :], T.hi2[b0, :], A.add).then_inc(sem.k3, 1)
    V.tensor_copy(T.slotown[blocks[1], :], T.slotr[b0, :]).then_inc(sem.vslot, 1)
    V.wait_ge(sem.k3, 2)
    V.transpose(T.placet[b0, :], T.place[b0, :]).then_inc(sem.k4, 1)
    V.tensor_copy(T.slotown[blocks[2], :], T.slotr[b0, :]).then_inc(sem.vslot, 1)
    V.wait_ge(sem.k4, 1)
    for k, b in enumerate(blocks):
        V.tensor_copy(T.placeu[b, :], T.placet[b0, 8 * (k // 2):8 * (k // 2) + 8]).then_inc(sem.k5, 1)
    V.tensor_copy(T.slotown[blocks[3], :], T.slotr[b0, :]).then_inc(sem.vslot, 1)
    V.wait_ge(sem.k5, 4)
    V.wait_ge(sem.ldown, 64)
    V.wait_ge(sem.szero, 3)
    V.tensor_copy(T.invrow[:].indirect(T.placeu[:]), T.ownrow[:]).then_inc(sem.scat, 1)
    SY.wait_ge(sem.scat, 1)
    SY.dma_start(T.invw[:], T.invrow[0:128:16, :]).then_inc(sem.ldinv, 16)
    V.wait_ge(sem.ve, 1)
    for b in range(4):
        make_e(b)

    asks = [[like], [unlike, mate] if fwd else [mate, unlike], grp["b"], grp["p"]]

    def engines(i, q):
        return on if q == mate else off if i < 2 else half(asks[i].index(q))

    g.wait_ge(sem.vreq, 4)
    for i in range(4):
        ts = []
        for q in asks[i]:
            k = 0 if i == 0 else pos(r) if i > 1 else (1 - pos(q) if q == mate else pos(q))
            ts.append(write(q, engines(i, q), T.req[:, LC * q:LC * q + LC], T["l%d" % i][:, LC * k:LC * k + LC], sem["lst%d" % i]))
        fused(ts)
    g.wait_ge(sem.vslot, 4)
    fused([write_core(helper(r), half(0, on), T.slotown[:], T.slotoff[:], sem.lston),
           write(mate, half(1, on), T.slotown[:], T.sloton[:], sem.lston)])

    def gather(eng, out, src, s, scale=None):
        if eng == "v":
            if scale is None:
                V.tensor_copy(out, src).then_inc(s, 1)
            else:
                V.tensor_scalar(out, src, scale, None, A.mult).then_inc(s, 1)
        elif scale is None:
            SC.activation(out, src, COPY).then_inc(s, 1)
        else:
            SC.activation(out, src, COPY, scale=scale).then_inc(s, 1)

    def xcols(t, offs):
        return T.xs[:, t:2048].indirect(offs)

    def own_cols(eng, a, n, t, s):
        gather(eng, T.acol[:, W * t + a:W * t + a + n], xcols(t, T.inv[:, a // 16:(a + n) // 16]), s, 0.5)

    SC.wait_ge(sem.vself, 1)
    SC.wait_ge(sem.ldx, 16)
    for t in range(4):
        gather("s", T.ask[:, 4 * col["own"] + t:4 * (col["own"] + CAP):4], xcols(t, T.selfoff[:, 0:LC]), sem.gself)
    V.wait_ge(sem.ldx, 16)
    V.wait_ge(sem.gself, 4)
    starts = [col["like"], min(col["unlike"], col["mate"]), col["b"], col["p"]]
    for eng, q in (("v", V), ("s", SC)):
        for i in range(4):
            n = len(asks[i])
            q.wait_ge(sem["lst%d" % i], sum(len(engines(i, s)) for s in asks[i]))
            for t in ((0, 1) if eng == "v" else (2, 3)):
                gather(eng, T.ask[:, 4 * starts[i] + t:4 * (starts[i] + n * CAP):4], xcols(t, T["l%d" % i][:, 0:n * LC]),
                       sem["g%s%d" % (eng, i)])
            if eng == "v":
                V.wait_ge(sem["gv%d" % i], 2)
                V.wait_ge(sem["gs%d" % i], 2)
                a, wide = tiles[i]
                o = t1 if i == 1 else 0
                V.quantize_mx(T["f%d" % i][:, o:o + wide], T["f%ds" % i][:, o:o + wide],
                              T.ask[:, 4 * a:4 * (a + wide)]).then_inc(sem["q%d" % i], 1)
                if i == 2:
                    V.wait_ge(sem.ldinv, 16)
                    V.tensor_tensor(T.invs[0:64, :], T.invw[0:64, :], T.invw[64:128, :], A.add).then_inc(sem.vsum, 1)
                    V.wait_ge(sem.vsum, 1)
                    for k in range(2):
                        V.tensor_scalar(T.inv[64 * k:64 * k + 64, :], T.invs[0:64, :], 4, None, A.mult).then_inc(sem.vinv, 1)
    slot0 = {c: CAP * grp[c][0] for c in GROUPS}
    V.wait_ge(sem.vinv, 2)
    own_cols("v", min(slot0["b"], slot0["p"]), 2 * G, 0, sem.ownv)
    SC.wait_ge(sem.vinv, 2)
    for c in GROUPS:
        for t in range(0 if c in "ga" else 1, 4):
            own_cols("s", slot0[c], G, t, sem["ac%s%d" % (c, t)])

    for i in range(4):
        g.wait_ge(sem["q%d" % i], 1)
        for plane in (False, True):
            ts = []
            for k, q in enumerate(asks[i]):
                src = piece("f%d" % i, plane, starts[i] - tiles[i][0] + (t1 if i == 1 else 0) + CAP * k, CAP)
                if q == mate:
                    dst, s = piece("f1", plane, mate_at(q), CAP), sem.fdg
                else:
                    dst, s = piece("f%d" % (i if i > 1 else 0), plane, 128 + CAP * pos(r), CAP), sem["fd" + "aabp"[i]]
                ts.append(write(q, engines(i, q), src, dst, s))
            fused(ts)

    win = {"g": ("f1", 4 * CAP - 128, PAD) if fwd else ("f1", 0, 0), "a": ("f0", G, PAD), "b": ("f2", G, PAD), "p": ("f3", G, PAD)}
    PE.wait_ge(sem.veq, 4)
    for j, c in enumerate(GROUPS):
        name, a, skip = win[c]
        PE.wait_ge(sem["q" + name[1]], 1)
        PE.wait_ge(sem["fd" + c], {"g": 2 * len(on), "a": 4 * len(off)}.get(c, 2 * len(off)))
        if j >= 2:
            PE.wait_ge(sem["add" + GROUPS[j - 2]], 4)
        hc = PAD + G * j
        for b in range(4):
            bank = T["ps%d" % (4 * (j % 2) + b)]
            PE.matmul_mx(bank[:, 0:128], T.eq[:, 128 * b:128 * b + 128], T.eqs[:, 128 * b:128 * b + 128],
                         T[name][:, a:a + 128], T[name + "s"][:, a:a + 128], True, True).then_inc(sem["mm%s%d" % (c, b)], 1)
            if c in "bp" and b == 0:
                V.wait_ge(sem.ownv, 1)
            else:
                V.wait_ge(sem["ac%s%d" % (c, b)], 1)
            V.wait_ge(sem["mm%s%d" % (c, b)], 1)
            V.tensor_tensor(T.h[:, 4 * hc + b:4 * (hc + G):4], bank[:, skip:skip + G],
                            T.acol[:, W * b + slot0[c]:W * b + slot0[c] + G], A.add).then_inc(sem["add" + c], 1)
        V.wait_ge(sem["add" + c], 4)
        m = "m" + c
        V.quantize_mx(T[m][:], T[m + "s"][:], T.h[:, 4 * (hc - PAD):4 * (hc + G)]).then_inc(sem[m], 1)
        g.wait_ge(sem[m], 1)
        at = G * j
        if c in "ga":
            for plane in (False, True):
                n = G if c == "g" else CAP
                ts = [write_core(helper(r), on, piece(m, plane, PAD, n), piece("offq", plane, at, n), sem["h" + c])]
                if c == "a":
                    ts.append(write(offn, off, piece(m, plane, PAD + n, n), piece("offq", plane, at + n, n), sem.loffa))
                fused(ts)
        for plane in (False, True):
            src = piece(m, plane, PAD, G)
            ts = [write(mate, on, src, piece("onq", plane, at, G), sem["lon" + c])]
            if c in "bp":
                ts.append(write(offn, off, src, piece("offq", plane, at, G), sem["loff" + c]))
            fused(ts)

    sec = {prv: 0, r: 1, nxt: 2}
    who = {"own": r, "on": mate, "off": offn}
    landed = {"ona": (("long", 2), ("lona", 2)), "offb": (("loffa", 2), ("loffb", 2)), "offa": (("lhelp", 4),)}

    def ycols(q, a, b):
        return slice(S * sec[q] + a, S * sec[q] + b)

    def parts(y):
        return "ga" if y in ("ona", "offa") else y[-1]

    def pick(eng, st, name, tile, a, b):
        e, cols = (V if eng == "v" else SC), ycols(who[tile], a, b)
        e.wait_ge(sem.vslot if tile == "own" else sem["lst" + tile], {"own": 4, "on": len(on) // 2, "off": len(off)}[tile])
        for y in YS:
            if y[:-1] == tile:
                e.wait_ge(sem["c" + y], len(parts(y)))
        gather(eng, T.ysb[:, cols], T["y" + tile][:].indirect(T["slot" + tile][:, a // 16:b // 16]), sem["pk" + name])
        st.wait_ge(sem["pk" + name], 1)
        st.dma_start(T.y[:, cols], T.ysb[:, cols]).then_inc(sem["st" + name], 16)

    V.wait_ge(sem.ldw, 16)
    V.quantize_mx(T.wq[:], T.wqs[:], T.ws[:]).then_inc(sem.vwq, 1)
    PE.wait_ge(sem.vwq, 1)
    PE.wait_ge(sem.mp, 1)
    for j, y in enumerate(YS):
        tile, c = y[:-1], y[-1]
        wide = max(G * len(parts(y)), 128)
        end = G * (GROUPS.index(c) + 1)
        if tile == "own":
            PE.wait_ge(sem["m" + c], 1)
            codes, scales = T["m" + c][:], T["m" + c + "s"][:]
        else:
            for s, n in landed.get(y, (("l" + y, 2),)):
                PE.wait_ge(sem[s], n * len(on if tile == "on" else off))
            codes, scales = T[tile + "q"][:, end - wide:end], T[tile + "qs"][:, end - wide:end]
        if j >= 8:
            PE.wait_ge(sem["c" + YS[j - 8]], 1)
        bank = T["ps%d" % (j % 8)]
        PE.matmul_mx(bank[:, 0:wide], T.wq[:], T.wqs[:], codes, scales, True, True).then_inc(sem["y" + y], 1)
        eng = "v" if tile == "own" else "s"
        (V if eng == "v" else SC).wait_ge(sem["y" + y], 1)
        for k, p in enumerate(reversed(parts(y))):
            at = CAP * groups(who[tile])[p][0]
            gather(eng, T["y" + tile][:, at:at + G], bank[:, wide - G * (k + 1):wide - G * k], sem["c" + y])
        if y == "ownp":
            pick("v", SY, "own", "own", 0, S)
        if y == "onp":
            pick("v", SY, "on", "on", 0, S)
    pick("v", SY, "off0", "off", 0, 128)
    pick("s", SC, "off1", "off", 128, S)

    g.wait_ge(sem.loc, sent[0])
    for name in PICKS:
        (SC if name == "off1" else SY).wait_ge(sem["st" + name], 16)
